import numpy as np, ml_dtypes
CORES = [36,164,52,180,100,228,116,244]
N = 8
BF = ml_dtypes.bfloat16
def gentries(a):
    return np.ascontiguousarray(a.reshape(8, 16, -1).transpose(0, 2, 1)).reshape(8, -1)
def gtable(e):
    e = np.asarray(e); return np.ascontiguousarray(e.reshape(8, -1, 16).transpose(0, 2, 1)).reshape(128, -1).astype(np.int32)
W, I, J, A, B, P, RO = 2048, 1024, 768, 4, 16, 128, 4
def column(i, j):
    return ((((2 * i + 1) * (2 * j + 1)) >> 5) + 37 * i + j) & (W - 1)
def sized(rng, n, lo, hi, noise):
    b = np.exp2(lo + (hi - lo) * rng.random((N, 8, 1, n), dtype=np.float32))
    return (b * np.exp2(noise * (2 * rng.random((N, 8, 16, n), dtype=np.float32) - 1))).astype(np.int64)
def parts(rng):
    v = np.minimum(np.maximum(sized(rng, W, 2.6, 6.8, 0.5), 1), 127)
    rl = rng.integers(0, J, (N, 8, 16, I)); cl = rng.integers(0, I, (N, 8, 16, J))
    i = rng.integers(0, I, (N, 8, P)); j = rng.integers(0, J, (N, 8, P))
    return v, rl, cl, i, j, np.minimum(sized(rng, P, 1.0, 6.0, 0.5), 127)
def pack(v, rl, cl, i, j, z):
    return {"fig": np.ascontiguousarray(v.reshape(N, 128, W)).astype(np.float32).astype(BF), "rmate": np.ascontiguousarray(rl.reshape(N, 128, I)).astype(np.int32), "cmate": np.ascontiguousarray(cl.reshape(N, 128, J)).astype(np.int32),
            "prow": np.stack([gtable(a) for a in i]), "pcol": np.stack([gtable(a) for a in j]), "need": np.ascontiguousarray(z.reshape(N, 128, P)).astype(np.float32).astype(BF)}
def some(rng, good, free):
    n = np.flatnonzero(good & free)
    if len(n) == 0: n = np.flatnonzero(free)
    return n[rng.integers(0, len(n), 128)]
def fill(rng, v, rl, cl, i, j, z, g):
    v[:, g] = 40 + np.argsort(rng.random((N, 16, W)), axis=1); z[:, g] = 0
    seen = np.zeros((N, W), bool); rows = np.zeros((N, I), bool); cols = np.zeros((N, J), bool); ai = np.arange(I); aj = np.arange(J)
    for q in range(N):
        i[q, g] = rng.permutation(I)[:P]; j[q, g] = rng.permutation(J)[:P]; rows[q, i[q, g]] = True; cols[q, j[q, g]] = True
    x = np.array(i[:, g]); y = np.array(j[:, g])
    for t in range(RO):
        if t == RO - 1: rows[:] = False; cols[:] = False
        nx = np.zeros_like(x); ny = np.zeros_like(y)
        for q in range(N):
            to = (q + 1 + t % 3) % N
            for k in range(P):
                a, b = int(x[q, k]), int(y[q, k])
                u = some(rng, ~seen[q][column(a, aj)], ~cols[to]); w = some(rng, ~seen[q][column(ai, b)], ~rows[to])
                c = np.stack([column(a, u), column(w, b), column(w, u)])
                n = int(np.argmax(~seen[q][c[2]] & (c[0] != c[1]) & (c[0] != c[2]) & (c[1] != c[2])))
                seen[q, c[:, n]] = True; cols[to, u[n]] = True; rows[to, w[n]] = True
                rl[q, g, :, a] = u[n]; cl[q, g, :, b] = w[n]; nx[to, k] = w[n]; ny[to, k] = u[n]
        x, y = nx, ny
def setup_inputs(rng):
    return pack(*parts(rng))
def setup_inputs_ties(rng):
    v, rl, cl, i, j, z = parts(rng)
    v = rng.choice(np.array([8, 16, 32, 64]), (N, 8, 1, W)) + np.zeros((1, 1, 16, 1), np.int64)
    low = (rng.random((N, 8, 1, W)) < 0.3) & (np.arange(16)[:, None] == rng.integers(0, 16, (N, 8, 1, W)))
    z = rng.choice(np.array([0, 1, 8, 9, 16, 32, 33, 64, 65]), (N, 8, 1, P)) + np.zeros((1, 1, 16, 1), np.int64)
    v = v - low; fill(rng, v, rl, cl, i, j, z, 3)
    return pack(v, rl, cl, i, j, z)
def setup_inputs_none(rng):
    v, rl, cl, i, j, z = parts(rng)
    h = int(rng.integers(0, 8)); z[int(rng.integers(0, N))] = 0; z[:, h] = 127; v[:, h] = np.minimum(v[:, h], 126)
    for g, a, b in (((h + 1) % 8, A - 1, B - 1), ((h + 2) % 8, 0, 0)):
        v[:, g] = np.minimum(v[:, g], 10); z[:, g] = rng.integers(20, 30, (N, 16, P))
        for q in range(N):
            for k in range(8):
                x, y = int(i[q, g, k]), int(j[q, g, k]); u, w = int(rl[q, g, a, x]), int(cl[q, g, b, y])
                for c in (column(x, u), column(w, y), column(w, u)): v[q, g, :, c] = 127
    return pack(v, rl, cl, i, j, z)
def setup_inputs_alike(rng):
    v, rl, cl, i, j, z = parts(rng); z = z // 4
    i[:, [0, 4]] = i[:, [0, 4], :1]; j[:, [0, 4]] = j[:, [0, 4], :1]; z[:, [0, 4]] = z[:, [0, 4], :, :1]
    rl[:, [1, 5]] = rng.choice(np.array([0, 5, J - 1]), (N, 2, 16, I)); cl[:, [1, 5]] = rng.choice(np.array([0, 7, I - 1]), (N, 2, 16, J))
    i[:, 2] = rng.choice(np.array([0, 1, I // 2, I - 1]), (N, P)); j[:, 2] = rng.choice(np.array([0, 1, J // 2, J - 1]), (N, P))
    rl[:, 6] = rl[:, 6, :1]; cl[:, 6] = cl[:, 6, :1]
    for q in range(N):
        rl[q, 7, 0, i[q, 7]] = j[q, 7]; cl[q, 7, 0, j[q, 7]] = i[q, 7]
        cl[q, 4, :, int(j[q, 4, 0])] = int(i[q, 4, 0])
    z[:, 4] = 0
    rl[:, 3] = np.where(rng.random((N, 16, I)) < 0.5, rng.choice(np.array([0, J - 1]), (N, 16, I)), rl[:, 3])
    cl[:, 3] = np.where(rng.random((N, 16, J)) < 0.5, rng.choice(np.array([0, I - 1]), (N, 16, J)), cl[:, 3])
    i[:, 3] = np.where(rng.random((N, P)) < 0.5, rng.choice(np.array([0, I - 1]), (N, P)), i[:, 3])
    j[:, 3] = np.where(rng.random((N, P)) < 0.5, rng.choice(np.array([0, J - 1]), (N, P)), j[:, 3])
    return pack(v, rl, cl, i, j, z)
def setup_inputs_late(rng):
    v, rl, cl, i, j, z = parts(rng); z = z // 4
    for g in range(8):
        s = rng.permutation(16)
        for q in range(N):
            a, b = int(s[q % 2]), int(s[1 - q % 2])
            v[q, g, a] = np.minimum(v[q, g, a], 12); z[q, g, a] = rng.integers(13, 30, P); z[q, g, b] = np.minimum(z[q, g, b], 6)
    return pack(v, rl, cl, i, j, z)
def setup_inputs_spread(rng):
    v, rl, cl, i, j, z = parts(rng)
    v = np.minimum(np.maximum(sized(rng, W, 0.0, 7.3, 0.3), 1), 127)
    z = np.minimum(sized(rng, P, -1.0, 7.2, 0.2), 127)
    v[:, 2] = rng.integers(123, 128, (N, 16, W)); z[:, 2] = np.minimum(z[:, 2], 60)
    v[:, 5] = np.where(rng.random((N, 1, W)) < 0.5, 127, 1); z[:, 5] = 127
    return pack(v, rl, cl, i, j, z)
def check_inputs(d):
    bad = []
    for k, lo, hi in (("fig", 1, 127), ("rmate", 0, J - 1), ("cmate", 0, I - 1), ("prow", 0, I - 1), ("pcol", 0, J - 1), ("need", 0, 127)):
        v = np.asarray(d[k]).astype(np.float64)
        if not (np.all(v >= lo) and np.all(v <= hi) and np.all(v == np.floor(v))): bad.append("range of " + k)
    return bad
def look(h, c, z):
    m = c.shape[1]; v = np.take_along_axis(h, c.reshape(8, 1, m * P), 2).reshape(8, 16, m, P)
    return np.all(np.abs(v) >= z[:, :, None, :], axis=1), np.sum(np.maximum(v, 0), axis=1)
def reference(fig, rmate, cmate, prow, pcol, need):
    h = fig.astype(np.float32).astype(np.int32).reshape(N, 8, 16, W); z = need.astype(np.float32).astype(np.int32).reshape(N, 8, 16, P)
    rm = rmate.astype(np.int64).reshape(N, 8, 16, I); cm = cmate.astype(np.int64).reshape(N, 8, 16, J)
    i = np.stack([gentries(a) for a in prow]).astype(np.int64); j = np.stack([gentries(a) for a in pcol]).astype(np.int64)
    cost = np.zeros((N, 8, RO, P), np.float32); gi = np.arange(8)[:, None] + np.zeros((1, P), np.int64)
    for t in range(RO):
        ra = A * (t % (16 // A)); rb = B * (t % (16 // B)); sh = 1 + t % 3
        ni, nj, nz = [None] * N, [None] * N, [None] * N
        for q in range(N):
            x, y = i[q], j[q]
            jm = np.take_along_axis(rm[q][:, ra:ra + A], x[:, None, :], 2)
            im = np.take_along_axis(cm[q][:, rb:rb + B], y[:, None, :], 2)
            ok1, c1 = look(h[q], column(x[:, None, :], jm), z[q]); ok2, c2 = look(h[q], column(im, y[:, None, :]), z[q])
            ok3, c3 = look(h[q], column(im[:, None, :, :], jm[:, :, None, :]).reshape(8, A * B, P), z[q])
            ok = (ok1[:, :, None, :] & ok2[:, None, :, :]).reshape(8, A * B, P) & ok3
            total = (c1[:, :, None, :] + c2[:, None, :, :]).reshape(8, A * B, P) + c3
            total = np.where(ok, total, 2 ** 20)
            best = np.argmin(total, axis=1); good = np.any(ok, axis=1)
            cost[q, :, t] = np.where(good, np.take_along_axis(total, best[:, None, :], 1)[:, 0], -1)
            u = np.take_along_axis(jm, (best // B)[:, None, :], 1)[:, 0]; w = np.take_along_axis(im, (best % B)[:, None, :], 1)[:, 0]
            far = column(w, u); hit = np.zeros((8, W), bool)
            for c in (column(x, u), column(w, y), far): hit[gi[good], c[good]] = True
            size = np.abs(h[q]); fresh = np.take_along_axis(size, far[:, None, :], 2) >> 1
            h[q] = np.where(hit[:, None, :], -size, h[q])
            to = (q + sh) % N
            ni[to] = np.where(good, w, x); nj[to] = np.where(good, u, y); nz[to] = np.where(good[:, None, :], fresh, z[q])
        i = np.stack(ni); j = np.stack(nj); z = np.stack(nz)
    yp = np.stack([gtable(np.concatenate([i[q], j[q]], axis=1)) for q in range(N)])
    return {"yf": h.reshape(N, 128, W).astype(np.float32).astype(BF), "yp": yp.astype(np.float32), "yz": z.reshape(N, 128, P).astype(np.float32).astype(BF), "yc": cost.reshape(N, 8, RO * P)}

@@ -1,0 +1,445 @@
+from concourse.mybir import AluOpType as A, ActivationFunctionType as F
+
+N, W, ROUNDS = 8, 2048, 4
+SHIFT = 315
+BIG = float(2 ** 19)
+FLAG = float(2 ** 21)
+
+SPEC = {
+    "bfloat16": "WIN 2048 CW 2048 HZ 2688 HT 2048 ZR 2048 FD 10752 CD 10752 OL 3072 OHH 384 KA 128 ZB 2048 YF 2048 IOT 160 MOD16 128 MOD20 160 "
+                "DIV16 128 DIV4 128 IDb 128 BLK 128 W1F 128 W1A 128 B8 8 W8F 8 W8A 8 ONE 128 BA 512 BB 128 CB 512 CIT 160 ZS0 128 ZS1 128 ZS2 128 ZS3 128",
+    "float32": "UC 768 VJ 768 U2 128 U1 32 R 512 TT 128 MSC 128 MC 32 OH 160 PW 160 SC2 160 PP 16 EE 128 ZF 64 NG 16 LHF 48 SQ 384 YP 16 YC 128 CK 128 pF 4 "
+               "cc 16 IDf 128 WIT 160 MK 16 MS 8 DRM 128 DRS 160 KC 32 KM0 24 KM1 24 KM2 24 KM3 24 KR0 24 KR1 24 KR2 24 KRX 24",
+    "int32": "CM 768 FC 768 FX 768 PR 16 XI 544 XJ 544 MI32 16 LI 8 ZI 16 KI 32 XC 24 LHI 48 CKI 64 CI 384 pI 4 RW0 1024 RW1 1024 RW2 1024 RW3 1024 "
+             "MSG0 16 MSG1 16 MSG2 16 MSG3 16 MR0 16 MR1 16 MR2 16 MR3 16",
+    "float16": "G16 128 SEL 512 SV1 512 SU1 512 WJT 160",
+    "uint16": "NL 16 LST 672 OFF 8",
+}
+PSUM = ("A0", "A1", "A2", "A3", "S2", "VB", "MI", "HH")
+SCRATCH = {n: ("psum", [128, 512], "float32") for n in PSUM}
+for _ty, _l in SPEC.items():
+    _l = _l.split()
+    for _n, _c in zip(_l[::2], _l[1::2]):
+        SCRATCH[_n] = ("sbuf", [128, int(_c)], _ty)
+SEMAPHORES = ["qv", "qs", "qt", "qg", "dl", "dc", "dd", "df", "dn", "dr0", "dr1", "dr2", "dr3", "oy0", "oy1", "oy2", "oy3", "oc", "op", "oz"] + \
+    [p + str(t) for p in ("rn", "rz", "rk", "ln", "lz", "lk") for t in range(ROUNDS)]
+CHUNKS = [("f2", 544, 128, 0), ("f1", 512, 32, 2048), ("a0", 0, 128, 2560), ("a1", 128, 128, 4608), ("a2", 256, 128, 6656), ("a3", 384, 128, 8704)]
+
+
+def rank_program(g, core, T, topo):
+    rank = T.rank_of(core)
+    if rank is None:
+        return
+    queues = {"v": g.vector, "s": g.scalar, "t": g.tensor, "g": g, "y": g.sync}
+    acc, cnt, final = {}, {}, {}
+    known = {q: {} for q in "vstgyx"}
+
+    def overlap(a, b):
+        if max(a[1], b[1]) >= min(a[2], b[2]):
+            return False
+        return a[3] != b[3] or a[3] == 1 or (a[1] - b[1]) % a[3] == 0
+
+    def before(q, reads, writes):
+        deps = {}
+        for kind, regs in (("r", reads), ("w", writes)):
+            for r in regs:
+                for k2, r2, q2, ev, clk in acc.get(r[0], ()):
+                    both = kind == "r" and k2 == "r"
+                    if r[0] in PSUM:
+                        if q == q2 and (q == "t" or both or not overlap(r, r2)):
+                            continue
+                    elif both or not overlap(r, r2):
+                        continue
+                    if known[q].get(ev[0], 0) < ev[1] and (ev[0] not in deps or deps[ev[0]][0] < ev[1]):
+                        deps[ev[0]] = (ev[1], clk)
+        for s in sorted(deps):
+            if not any(s2 != s and deps[s2][1].get(s, 0) >= deps[s][0] for s2 in deps):
+                queues[q].wait_ge(T.sem[s], deps[s][0])
+        for s in deps:
+            for s2, v in list(deps[s][1].items()) + [(s, deps[s][0])]:
+                known[q][s2] = max(known[q].get(s2, 0), v)
+
+    def after(q, reads, writes, ev):
+        clk = dict(known[q])
+        clk[ev[0]] = max(clk.get(ev[0], 0), ev[1])
+        for kind, regs in (("r", reads), ("w", writes)):
+            for r in regs:
+                keep = []
+                for e in acc.get(r[0], ()):
+                    inside = r[1] <= e[1][1] and e[1][2] <= r[2] and (r[3] == 1 or (r[3] == e[1][3] and (r[1] - e[1][1]) % r[3] == 0))
+                    if not (inside and (kind == "w" or (e[0] == "r" and e[2] == q))):
+                        keep.append(e)
+                acc[r[0]] = keep + [(kind, r, q, ev, clk)]
+
+    def emit(q, call, reads, writes):
+        before(q, reads, writes)
+        s = "q" + q
+        cnt[s] = cnt.get(s, 0) + 1
+        call().then_inc(T.sem[s], 1)
+        final[s] = cnt[s]
+        after(q, reads, writes, (s, cnt[s]))
+
+    def dmas(q, sem, moves):
+        total = 16 * len(moves)
+        for out, in_ in moves:
+            before(q, in_[1], out[1])
+            queues[q].dma_start(out[0], in_[0]).then_inc(T.sem[sem], 16)
+        for out, in_ in moves:
+            after(q, in_[1], out[1], (sem, total))
+        final[sem] = total
+
+    def S(name, a, b, step=1, p0=0, p1=128):
+        t = T[name]
+        return (t[p0:p1, a:b] if step == 1 else t[p0:p1, a:b:step], [(name, a, b, step)])
+
+    def B(name, i, n=128):
+        return S(name, n * i, n * i + n)
+
+    def X(ap):
+        return (ap, [])
+
+    def G(win, off):
+        return (win[0].indirect(off[0]), win[1] + off[1])
+
+    def sc(x):
+        return x[0] if isinstance(x, tuple) else x
+
+    def rg(*xs):
+        r = []
+        for x in xs:
+            r = r + (x[1] if isinstance(x, tuple) else [])
+        return r
+
+    def cp(out, in_):
+        emit("v", lambda: g.vector.tensor_copy(out[0], in_[0]), in_[1], out[1])
+
+    def tt(out, a, b, op):
+        emit("v", lambda: g.vector.tensor_tensor(out[0], a[0], b[0], op), a[1] + b[1], out[1])
+
+    def ts(out, a, s1, op0, s2=None, op1=None):
+        if op1 is None:
+            emit("v", lambda: g.vector.tensor_scalar(out[0], a[0], sc(s1), None, op0), rg(a, s1), out[1])
+        else:
+            emit("v", lambda: g.vector.tensor_scalar(out[0], a[0], sc(s1), sc(s2), op0, op1), rg(a, s1, s2), out[1])
+
+    def ms(out, c):
+        emit("v", lambda: g.vector.memset(out[0], c), [], out[1])
+
+    def scan(out, a, b, init, op0, op1):
+        emit("v", lambda: g.vector.tensor_tensor_scan(out[0], a[0], b[0], init, op0, op1), rg(a, b), out[1])
+
+    def act(out, in_, func=F.Copy, bias=0.0, scale=1.0):
+        emit("s", lambda: g.scalar.activation(out[0], in_[0], func, bias=sc(bias), scale=sc(scale)), rg(in_, bias, scale), out[1])
+
+    def mm(out, lhsT, rhs, start, stop):
+        emit("t", lambda: g.tensor.matmul(out[0], lhsT[0], rhs[0], start, stop), lhsT[1] + rhs[1], out[1])
+
+    def iota(out, pattern, base=0, cm=0):
+        if SCRATCH[out[1][0][0]][2] == "int32":
+            emit("g", lambda: g.iota(out[0], pattern, base, cm), [], out[1])
+        else:
+            emit("g", lambda: g.iota(out[0], pattern, base, cm, allow_small_or_imprecise_dtypes=True), [], out[1])
+
+    def send(out, src, dst, rsem, lsem):
+        before("g", src[1], [])
+        rid, pid = topo.addr(dst, core)
+        g.remote_dma(out[0], src[0], T.sem[rsem], T.sem[lsem], pid, rid, topo.mask(core, dst))
+        final[lsem] = len(topo.engines(core, dst))
+
+    def recv(out, src, rsem):
+        final[rsem] = len(topo.engines(src, core))
+        after("x", [], out[1], (rsem, final[rsem]))
+
+    def load_mates(t):
+        n = "RW%d" % t
+        iota(B(n, 0, 1024), [[1, 1024]])
+        dmas("y", "dr%d" % t, [((T[n][16 * q:16 * q + 4, :], [(n, 0, 1024, 1)]), X(T.rmate[16 * q + 4 * t:16 * q + 4 * t + 4, :])) for q in range(8)])
+
+    dmas("y", "dl", [(S("PR", 0, 8), X(T.prow[:])), (S("PR", 8, 16), X(T.pcol[:]))])
+    dmas("y", "dc", [(B("CM", 0, 384), X(T.cmate[:, 0:384]))])
+    dmas("y", "dd", [(B("CM", 1, 384), X(T.cmate[:, 384:768]))])
+    dmas("s", "dn", [(S("HZ", W, W + 128), X(T.need[:]))])
+    iota(S("pI", 0, 1), [[0, 1]], 0, 1)
+    iota(B("IOT", 0, 160), [[1, 160]])
+    iota(B("DIV16", 0), [[1, 8], [0, 16]])
+    iota(B("DIV4", 0), [[1, 32], [0, 4]])
+    load_mates(0)
+    iota(S("VJ", 0, 768), [[2, 768]], 593)
+    iota(B("MOD16", 0), [[0, 8], [1, 16]])
+    iota(B("MOD20", 0, 160), [[0, 8], [1, 20]])
+    iota(S("ZB", 0, W), [[0, W]])
+    for t in range(1, ROUNDS):
+        load_mates(t)
+    PF, PG, PS = S("pF", 0, 1), S("pF", 1, 2), S("pF", 2, 3)
+
+    def cc(i):
+        return S("cc", i, i + 1)
+
+    ms(B("ONE", 0), 1.0)
+    ms(S("CB", 0, 512, 1, 0, 64), 4.0)
+    ms(S("CB", 0, 512, 1, 64, 128), 81.0 / 128)
+    ts(S("pI", 1, 2), S("pI", 0, 1), 4, A.logical_shift_right)
+    ts(S("pI", 2, 3), S("pI", 0, 1), 15, A.bitwise_and)
+    cp(S("pF", 0, 3), S("pI", 0, 3))
+    ts(B("BLK", 0), B("DIV16", 0), PG, A.is_equal)
+    ts(S("B8", 0, 8), S("IOT", 0, 8), PG, A.is_equal)
+    for a in range(4):
+        ts(cc(a), PS, float(a), A.is_equal)
+    ts(cc(4), PS, 4.0, A.is_ge, 200.0, A.mult)
+    ts(cc(5), PS, 15.0, A.is_lt, 200.0, A.mult)
+    ts(cc(6), PG, 4.0, A.mult, PF, A.add)
+    tt(cc(7), cc(4), PF, A.add)
+    ts(cc(8), PG, 4.0, A.mult, cc(5), A.add)
+    ts(cc(9), cc(4), 2.0, A.mult, cc(6), A.add)
+    for a in range(4):
+        ts(B("SEL", a), B("BLK", 0), cc(a), A.mult)
+    for c in range(4):
+        ts(B("SV1", c), B("IOT", 0), 4.0 * c, A.subtract, cc(7), A.is_equal)
+        ts(B("SU1", c), B("DIV4", 0), float(c), A.subtract, cc(8), A.is_equal)
+    cp(S("NL", 0, 16), S("PR", 0, 16))
+    for h in range(2):
+        ts(B("UC", h, 384), B("CM", h, 384), 4.0, A.mult, 34.0, A.add)
+        tt(B("FX", h, 384), B("UC", h, 384), B("VJ", h, 384), A.mult)
+        ts(B("FC", h, 384), B("FX", h, 384), 6, A.logical_shift_right, 2047, A.bitwise_and)
+    act(S("W8F", 0, 8), S("B8", 0, 8), F.Copy, 0.0, BIG)
+    act(S("W8A", 0, 8), S("B8", 0, 8), F.Copy, 0.0, 64.0)
+    act(B("W1F", 0), B("BLK", 0), F.Copy, 0.0, BIG)
+    act(B("W1A", 0), B("BLK", 0), F.Copy, 0.0, 64.0)
+    for a in range(4):
+        act(B("BA", a), B("BLK", 0), F.Copy, a / 8.0, 0.0)
+    dmas("s", "df", [(S("WIN", SHIFT, W), X(T.fig[:, 0:W - SHIFT])), (S("WIN", 0, SHIFT), X(T.fig[:, W - SHIFT:W]))])
+    act(B("BB", 0), B("MOD16", 0), F.Copy, 0.0, 1.0 / 128)
+
+    def late_constants():
+        ts(B("IDb", 0), B("IOT", 0), PF, A.is_equal)
+        ts(B("WIT", 0, 160), B("IOT", 0, 160), cc(6), A.is_equal, 256.0, A.mult)
+        ts(B("WJT", 0, 160), B("IOT", 0, 160), 16.0, A.subtract, cc(9), A.is_equal)
+        ms(S("cc", 10, 11, 1, 0, 64), 32768.0)
+        ms(S("cc", 10, 11, 1, 64, 128), -120.0)
+        ts(B("CIT", 0, 160), B("MOD20", 0, 160), 16.0, A.is_lt, cc(10), A.mult)
+        ts(S("MK", 0, 16), S("IOT", 0, 16), PS, A.is_equal)
+        ts(S("MS", 0, 8), S("IOT", 0, 8), PG, A.is_equal)
+        ts(B("DRM", 0), B("MOD16", 0), 0.0, A.is_equal, float(2 ** 26), A.mult)
+        ts(B("DRS", 0, 160), B("MOD20", 0, 160), 0.5, A.is_gt)
+        ts(S("PP", 0, 8), S("PR", 0, 8), 1024.0, A.mult, 1024.0, A.add)
+        for t in range(ROUNDS):
+            ts(S("ZF", 32 + 8 * t, 40 + 8 * t), S("IOT", 0, 8), 16.0, A.mult, W + 128.0 * t, A.add)
+        tt(S("PP", 8, 16), S("PP", 0, 8), S("PR", 8, 16), A.add)
+        ts(S("KC", 0, 32), S("ZF", 32, 64), PS, A.add)
+        for m in range(8):
+            act(B("EE", m, 16), S("MK", 0, 16), F.Copy, 0.0, S("PP", 8 + m, 9 + m))
+        mm(S("HH", 448, 456), B("EE", 0), S("MS", 0, 8), True, True)
+        for h in range(16):
+            mm(B("HH", h, 8), B("WIN", h), S("B8", 0, 8), True, True)
+        act(S("HT", 0, W), S("WIN", 0, W), F.Copy, -0.25, 0.5)
+        act(B("IDf", 0), B("IDb", 0))
+
+    def late_places():
+        cp(S("KRX", 16, 24), S("HH", 448, 456))
+        ts(S("KI", 0, 8), S("KRX", 16, 24), 1024.0, A.subtract)
+        ts(S("KI", 8, 16), S("KI", 0, 8), 10, A.logical_shift_right, 1023, A.bitwise_and)
+        ts(S("KI", 16, 24), S("KI", 0, 8), 1023, A.bitwise_and)
+        ts(S("KRX", 0, 8), S("KI", 8, 16), 2.0, A.mult, 17.0, A.add)
+        ts(S("KRX", 8, 16), S("KI", 16, 24), 2.0, A.mult, 593.0, A.add)
+        ts(S("HZ", 0, W), S("HT", 0, W), 8388608.0, A.add, 8388608.0, A.subtract)
+        cp(S("CI", 0, 128), B("HH", 0))
+        ts(S("CI", 128, 256), S("CI", 0, 128), 2032, A.bitwise_and)
+        ts(S("CI", 256, 384), S("CI", 0, 128), 15, A.bitwise_and)
+        cp(S("ZB", 0, W, 16), S("CI", 128, 256))
+        cp(S("ZB", 1, W, 16), S("CI", 256, 384))
+
+    def vb_bias():
+        mm(S("VB", 0, 512), B("ONE", 0), S("CB", 0, 512), True, False)
+
+    def lists_a(t):
+        if t > 0:
+            cp(S("NL", 0, 16), S("MR%d" % (t - 1), 0, 16))
+        cp(B("G16", 0), G(B("RW%d" % t, 0, 1024), S("NL", 0, 8)))
+        cp(S("LST", 544, 672), G(S("FC", 0, 768), S("NL", 8, 16)))
+        act(B("U2", 0), G(S("UC", 0, 768), S("NL", 8, 16)))
+        for a in range(4):
+            mm(B("VB", a), B("SEL", a), B("G16", 0), False, a == 3)
+        for c in range(4):
+            mm(S("MI", 0, 32), B("SU1", c), S("G16", c, 128, 4), c == 0, c == 3)
+        mm(S("MI", 32, 64), B("ONE", 0), S("CB", 0, 32), True, False)
+        for c in range(4):
+            mm(S("MI", 32, 64), B("SV1", c), S("G16", c, 128, 4), False, c == 3)
+
+    def lists_b():
+        for a in range(4):
+            tt(B("XI", a), B("U2", 0), B("VB", a), A.mult)
+        ts(S("U1", 0, 32), S("MI", 0, 32), 4.0, A.mult, 34.0, A.add)
+        tt(S("XI", 512, 544), S("U1", 0, 32), S("MI", 32, 64), A.mult)
+        ts(S("XJ", 0, 544), S("XI", 0, 544), 5, A.logical_shift_right, 2047, A.bitwise_and)
+        cp(S("LST", 0, 544), S("XJ", 0, 544))
+
+    def needs_s(t):
+        for b in range(0, 16, 2):
+            act(S("ZR", b, W, 16), S("HZ", W + 128 * t, W + 128 * t + 128))
+
+    def needs_v(t):
+        for b in range(1, 16, 2):
+            cp(S("ZR", b, W, 16), S("HZ", W + 128 * t, W + 128 * t + 128))
+
+    vb_bias()
+    lists_a(0)
+    needs_s(0)
+    lists_b()
+    needs_v(0)
+    for t in range(ROUNDS):
+        dst = T.cores[(rank + 1 + t % 3) % N]
+        src = T.cores[(rank - 1 - t % 3) % N]
+        last = t == ROUNDS - 1
+        kr = "KRX" if t == 0 else "KR%d" % (t - 1)
+        win = "WIN" if t == 0 else "CW"
+        zs = W + 128 * t
+
+        mm(B("S2", 0), B("ONE", 0), B("BB", 0), True, False)
+        for a in range(4):
+            mm(B("A%d" % a, 0), B("ONE", 0), B("BA", a), True, False)
+        for name, off, cols, pos in CHUNKS:
+            o, n = S("LST", off, off + cols), 16 * cols
+            act(S("CD", pos, pos + n), G(S(win, 0, W), o))
+            tt(S("FD", pos, pos + n), G(S("WIN", 0, W), o), S("ZR", 0, W, 4) if name == "f1" else S("ZR", 0, W), A.is_lt)
+            if name == "f1":
+                for a in range(4):
+                    mm(B("A%d" % a, 0), S("CD", pos + a, pos + n, 4), B("W1A", 0), False, False)
+                    mm(B("A%d" % a, 0), S("FD", pos + a, pos + n, 4), B("W1F", 0), False, False)
+                if t == 0:
+                    late_constants()
+                mm(S("MI", 64, 224), B("ONE", 0), B("CIT", 0, 160), True, False)
+                mm(S("MI", 64, 224), B("U2", 0), B("WIT", 0, 160), False, False)
+                mm(S("MI", 64, 224), B("G16", 0), B("WJT", 0, 160), False, True)
+                continue
+            bank = "S2" if name == "f2" else "A" + name[1]
+            for b in range(16):
+                mm(S(bank, b, 128, 16), S("FD", pos + b, pos + n, 16), S("W8F", 0, 8), False, False)
+            for b in range(16):
+                mm(S(bank, b, 128, 16), S("CD", pos + b, pos + n, 16), S("W8A", 0, 8), False, b == 15)
+            if name == "a0" and t == 0:
+                late_places()
+            if name == "a1":
+                act(B("R", 0), B("A0", 0))
+            if name == "a2":
+                tt(B("R", 1), B("R", 0), B("A1", 0), A.min)
+            if name == "a3":
+                tt(B("R", 2), B("R", 1), B("A2", 0), A.min)
+
+        tt(B("R", 3), B("R", 2), B("A3", 0), A.min)
+        tt(B("TT", 0), B("R", 3), B("S2", 0), A.add)
+        scan(B("MSC", 0), B("DRM", 0), B("TT", 0), float(2 ** 26), A.add, A.min)
+        m8 = S("MSC", 15, 128, 16)
+        ts(B("MC", t, 8), m8, BIG - 1, A.min, 1.0, A.add)
+        cp(S("MI32", 0, 8), m8)
+        for q in range(8):
+            o, i, col = S("OH", 20 * q, 20 * q + 16), B("TT", q, 16), S("MC", 8 * t + q, 8 * t + q + 1)
+            if q < 3:
+                ts(o, i, 1.0, A.add, col, A.is_equal)
+            else:
+                act(o, i, F.Relu, col, -1.0)
+        ts(S("MI32", 8, 16), S("MI32", 0, 8), 4, A.logical_shift_right, 3, A.bitwise_and)
+        for a in range(4):
+            ts(S("OH", 16 + a, 160, 20), S("MI32", 8, 16), float(a), A.is_equal)
+        tt(B("PW", 0, 160), B("OH", 0, 160), S("MI", 64, 224), A.mult)
+        scan(B("SC2", 0, 160), B("DRS", 0, 160), B("PW", 0, 160), 0.0, A.mult, A.add)
+        tt(S("PP", 8, 16), S("SC2", 19, 160, 20), S(kr, 16, 24), A.max)
+        for q in range(8):
+            o, col = B("EE", q, 16), S("PP", 8 + q, 9 + q)
+            if q < 5:
+                ts(o, S("MK", 0, 16), col, A.mult)
+            else:
+                act(o, S("MK", 0, 16), F.Copy, 0.0, col)
+        LQ = S("HH", 448, 456)
+        mm(LQ, B("EE", 0), S("MS", 0, 8), True, True)
+        if not last:
+            vb_bias()
+        msg, km = "MSG%d" % t, "KM%d" % t
+        ts(S("KI", 0, 8), S("PP", 8, 16), 1024.0, A.subtract)
+        ts(S("NG", 0, 8), S("PP", 8, 16), FLAG, A.is_lt, 64.0, A.mult)
+        ts(S("KI", 8, 16), S("KI", 0, 8), 10, A.logical_shift_right, 1023, A.bitwise_and)
+        ts(S("KI", 16, 24), S("KI", 0, 8), 1023, A.bitwise_and)
+        ts(S(km, 0, 8), S("KI", 8, 16), 2.0, A.mult, 17.0, A.add)
+        ts(S(km, 8, 16), S("KI", 16, 24), 2.0, A.mult, 593.0, A.add)
+        tt(S("XC", 0, 8), S(kr, 0, 8), S(km, 8, 16), A.mult)
+        ts(S("LI", 0, 8), LQ, 1024.0, A.subtract)
+        tt(S("XC", 8, 16), S(km, 0, 8), S(kr, 8, 16), A.mult)
+        tt(S("XC", 16, 24), S(km, 0, 8), S(km, 8, 16), A.mult)
+        ts(S(msg, 0, 8), S("LI", 0, 8), 10, A.logical_shift_right, 1023, A.bitwise_and)
+        ts(S(msg, 8, 16), S("LI", 0, 8), 1023, A.bitwise_and)
+        send(S("MR%d" % t, 0, 16), S(msg, 0, 16), dst, "rn%d" % t, "ln%d" % t)
+        recv(S("MR%d" % t, 0, 16), src, "rn%d" % t)
+        ts(S("LHI", 24, 48), S("XC", 0, 24), 12, A.logical_shift_right, 15, A.bitwise_and)
+        ts(S("LHI", 0, 24), S("XC", 0, 24), 5, A.logical_shift_right, 127, A.bitwise_and)
+        ts(S("ZF", 8, 16), LQ, FLAG, A.is_lt)
+        for c in range(3):
+            tt(S("LHF", 24 + 8 * c, 32 + 8 * c), S("LHI", 24 + 8 * c, 32 + 8 * c), S("NG", 0, 8), A.add)
+        cp(S("LHF", 0, 24), S("LHI", 0, 24))
+        ts(S("ZF", 16, 24), S(msg, 0, 8), 2.0, A.mult, 17.0, A.add)
+        ts(S("ZF", 24, 32), S(msg, 8, 16), 2.0, A.mult, 593.0, A.add)
+        tt(S("ZI", 0, 8), S("ZF", 16, 24), S("ZF", 24, 32), A.mult)
+        ts(S("ZI", 8, 16), S("ZI", 0, 8), 5, A.logical_shift_right, 2047, A.bitwise_and)
+        tt(S("ZF", 32, 40), S("ZF", 8, 16), B("KC", t, 8), A.mult)
+        tt(S("ZF", 40, 48), S("ZI", 8, 16), S("ZF", 32, 40), A.max)
+        cp(S("OFF", 0, 8), S("ZF", 40, 48))
+        cp(B("ZS%d" % t, 0), G(S("HZ", 0, zs + 128), S("OFF", 0, 8)))
+        send(S("HZ", zs + 128, zs + 256), B("ZS%d" % t, 0), dst, "rz%d" % t, "lz%d" % t)
+        recv(S("HZ", zs + 128, zs + 256), src, "rz%d" % t)
+        for h in range(2):
+            for q in range(4 * h, 4 * h + 4):
+                for c in range(3):
+                    n, m = 3 * q + c, 8 * c + q
+                    act(B("SQ", n, 16), S("IOT", 0, 16), F.Square, S("LHF", 24 + m, 25 + m), -1.0)
+                    ts(B("OL", n), B("IOT", 0), S("LHF", m, m + 1), A.is_equal)
+            act(B("OHH", h, 192), B("SQ", h, 192), F.Relu, 4096.0, -4096.0)
+            for q in range(4 * h, 4 * h + 4):
+                for c in range(3):
+                    n = 3 * q + c
+                    mm(S("HH", q, 128, 8), B("OL", n), B("OHH", n, 16), c == 0, c == 2)
+        if not last:
+            ts(S("NG", 8, 16), S("PP", 8, 16), FLAG, A.is_ge, -FLAG, A.mult)
+            tt(S(km, 16, 24), S("PP", 8, 16), S("NG", 8, 16), A.add)
+            send(S("KR%d" % t, 0, 24), S(km, 0, 24), dst, "rk%d" % t, "lk%d" % t)
+            recv(S("KR%d" % t, 0, 24), src, "rk%d" % t)
+            lists_a(t + 1)
+            needs_s(t + 1)
+        else:
+            ts(S("CK", 0, 32), S("MC", 0, 32), 1.0, A.subtract)
+            ts(S("CK", 32, 64), S("MC", 0, 32), BIG, A.is_lt)
+            cp(S("CKI", 0, 32), S("CK", 0, 32))
+            ts(S("CKI", 32, 64), S("CKI", 0, 32), 6, A.logical_shift_right)
+            ts(S("CK", 64, 96), S("CKI", 32, 64), 1.0, A.add)
+            tt(S("CK", 96, 128), S("CK", 64, 96), S("CK", 32, 64), A.mult)
+            ts(S("CK", 0, 32), S("CK", 96, 128), 1.0, A.subtract)
+        for d in range(1 if last else 2):
+            tt(S("ZB", d, W, 16), S("ZB", d, W, 16), B("HH", 0), A.subtract)
+        if last:
+            ts(B("KA", 0), S("ZB", 0, W, 16), 0.0, A.is_gt)
+            for s in range(16):
+                if s % 3 == 2:
+                    act(S("ZB", s, W, 16), B("KA", 0), F.Copy, -1.0, 2.0)
+                else:
+                    ts(S("ZB", s, W, 16), B("KA", 0), 2.0, A.mult, -1.0, A.add)
+        for h in range(16):
+            mm(B("A%d" % (h // 4), h % 4), B("ZB", h), B("IDb", 0), True, True)
+        if last:
+            for h in range(4):
+                tt(B("YF", h, 512), B("WIN", h, 512), S("A%d" % h, 0, 512), A.mult)
+                if h == 0:
+                    dmas("y", "oy0", [(X(T.yf[:, W - SHIFT:W]), S("YF", 0, SHIFT)), (X(T.yf[:, 0:512 - SHIFT]), S("YF", SHIFT, 512))])
+                else:
+                    dmas("y", "oy%d" % h, [(X(T.yf[:, 512 * h - SHIFT:512 * h + 512 - SHIFT]), B("YF", h, 512))])
+        else:
+            for h in range(3):
+                act(B("CW", h, 512), S("A%d" % h, 0, 512), F.Relu)
+            lists_b()
+            needs_v(t + 1)
+            ts(B("CW", 3, 512), S("A3", 0, 512), 0.0, A.max)
+
+    mm(S("S2", 0, 128, 1, 0, 32), S("CK", 0, 32), B("IDf", 0), True, True)
+    act(S("YC", 0, 128, 1, 0, 32), S("S2", 0, 128, 1, 0, 32))
+    cp(S("YP", 0, 16), S("MR3", 0, 16))
+    dmas("s", "oc", [(X(T.yc[:, 128 * t:128 * t + 128]), S("YC", 0, 128, 1, 8 * t, 8 * t + 8)) for t in range(ROUNDS)])
+    dmas("s", "oz", [(X(T.yz[:]), S("HZ", W + 512, W + 640))])
+    dmas("s", "op", [(X(T.yp[:]), S("YP", 0, 16))])
+    for s in sorted(final):
+        g.wait_ge(T.sem[s], final[s])

@@ -7,12 +7,13 @@ FLAG = float(2 ** 21)
 
 SPEC = {
     "bfloat16": "WIN 2048 CW 2048 HZ 2688 HT 2048 ZR 2048 FD 10752 CD 10752 OL 3072 OHH 384 KA 128 ZB 2048 YF 2048 IOT 160 MOD16 128 MOD20 160 "
-                "DIV16 128 DIV4 128 IDb 128 BLK 128 W1F 128 W1A 128 B8 8 W8F 8 W8A 8 ONE 128 BA 512 BB 128 CB 512 CIT 160 ZS0 128 ZS1 128 ZS2 128 ZS3 128",
-    "float32": "UC 768 VJ 768 U2 128 U1 32 R 512 TT 128 MSC 128 MC 32 OH 160 PW 160 SC2 160 PP 16 EE 128 ZF 64 NG 16 LHF 48 SQ 384 YP 16 YC 128 CK 128 pF 4 "
-               "cc 16 IDf 128 WIT 160 MK 16 MS 8 DRM 128 DRS 160 KC 32 KM0 24 KM1 24 KM2 24 KM3 24 KR0 24 KR1 24 KR2 24 KRX 24",
-    "int32": "CM 768 FC 768 FX 768 PR 16 XI 544 XJ 544 MI32 16 LI 8 ZI 16 KI 32 XC 24 LHI 48 CKI 64 CI 384 pI 4 RW0 1024 RW1 1024 RW2 1024 RW3 1024 "
+                "DIV16 128 DIV8 128 DIV4 128 IDb 128 BLK 128 W1F 128 W1A 128 B8 8 W8F 8 W8A 8 ONE 128 BA 512 BB 128 CB 512 CIT 640 CFL 160 "
+                "ZS0 128 ZS1 128 ZS2 128 ZS3 128",
+    "float32": "UC 768 VJ 768 VO 128 U2 128 U1 32 UP 128 SU3 512 R 512 TT 128 MSC 128 MC 32 OH 160 PW 160 SC2 160 PP 16 EE 128 ZF 64 NG 16 LHF 48 SQ 384 "
+               "YP 16 YC 128 CK 128 pF 4 cc 16 IDf 128 WIT 160 MK 16 MS 8 DRM 128 DRS 160 KC 32 KM0 24 KM1 24 KM2 24 KM3 24 KR0 24 KR1 24 KR2 24 KRX 24",
+    "int32": "CM 768 PR 16 XI 672 XJ 672 MI32 16 LI 8 ZI 16 KI 32 XC 24 LHI 48 CKI 64 CI 384 pI 4 RW0 1024 RW1 1024 RW2 1024 RW3 1024 "
              "MSG0 16 MSG1 16 MSG2 16 MSG3 16 MR0 16 MR1 16 MR2 16 MR3 16",
-    "float16": "G16 128 SEL 512 SV1 512 SU1 512 WJT 160",
+    "float16": "G16 128 SEL 512 SV1 512 SU1 512 SV3 256 WJT 160",
     "uint16": "NL 16 LST 672 OFF 8",
 }
 PSUM = ("A0", "A1", "A2", "A3", "S2", "VB", "MI", "HH")
@@ -23,7 +24,7 @@ for _ty, _l in SPEC.items():
         SCRATCH[_n] = ("sbuf", [128, int(_c)], _ty)
 SEMAPHORES = ["qv", "qs", "qt", "qg", "dl", "dc", "dd", "df", "dn", "dr0", "dr1", "dr2", "dr3", "oy0", "oy1", "oy2", "oy3", "oc", "op", "oz"] + \
     [p + str(t) for p in ("rn", "rz", "rk", "ln", "lz", "lk") for t in range(ROUNDS)]
-CHUNKS = [("f2", 544, 128, 0), ("f1", 512, 32, 2048), ("a0", 0, 128, 2560), ("a1", 128, 128, 4608), ("a2", 256, 128, 6656), ("a3", 384, 128, 8704)]
+CHUNKS = [("f2", 384, 128, 0), ("a0", 0, 128, 2560), ("a1", 128, 128, 4608), ("a2", 256, 128, 6656), ("f1", 512, 32, 2048), ("a3", 544, 64, 8704), ("a3", 608, 64, 9728)]
 
 
 def rank_program(g, core, T, topo):
@@ -37,7 +38,11 @@ def rank_program(g, core, T, topo):
     def overlap(a, b):
         if max(a[1], b[1]) >= min(a[2], b[2]):
             return False
-        return a[3] != b[3] or a[3] == 1 or (a[1] - b[1]) % a[3] == 0
+        if a[3] == b[3]:
+            return a[3] == 1 or (a[1] - b[1]) % a[3] == 0
+        if a[3] < b[3]:
+            a, b = b, a
+        return any(x in range(b[1], b[2], b[3]) for x in range(a[1], a[2], a[3]))
 
     def before(q, reads, writes):
         deps = {}
@@ -162,8 +167,9 @@ def rank_program(g, core, T, topo):
     iota(S("pI", 0, 1), [[0, 1]], 0, 1)
     iota(B("IOT", 0, 160), [[1, 160]])
     iota(B("DIV16", 0), [[1, 8], [0, 16]])
-    iota(B("DIV4", 0), [[1, 32], [0, 4]])
+    iota(B("DIV8", 0), [[1, 16], [0, 8]])
     load_mates(0)
+    iota(B("DIV4", 0), [[1, 32], [0, 4]])
     iota(S("VJ", 0, 768), [[2, 768]], 593)
     iota(B("MOD16", 0), [[0, 8], [1, 16]])
     iota(B("MOD20", 0, 160), [[0, 8], [1, 20]])
@@ -178,6 +184,9 @@ def rank_program(g, core, T, topo):
     ms(B("ONE", 0), 1.0)
     ms(S("CB", 0, 512, 1, 0, 64), 4.0)
     ms(S("CB", 0, 512, 1, 64, 128), 81.0 / 128)
+    ms(S("cc", 10, 14, 1, 64, 128), -120.0)
+    for t in range(ROUNDS):
+        ms(S("cc", 10 + t, 11 + t, 1, 0, 64), 32768.0 * (t + 1))
     ts(S("pI", 1, 2), S("pI", 0, 1), 4, A.logical_shift_right)
     ts(S("pI", 2, 3), S("pI", 0, 1), 15, A.bitwise_and)
     cp(S("pF", 0, 3), S("pI", 0, 3))
@@ -195,12 +204,29 @@ def rank_program(g, core, T, topo):
         ts(B("SEL", a), B("BLK", 0), cc(a), A.mult)
     for c in range(4):
         ts(B("SV1", c), B("IOT", 0), 4.0 * c, A.subtract, cc(7), A.is_equal)
+    ts(B("IDb", 0), B("IOT", 0), PF, A.is_equal)
+    ts(B("WIT", 0, 160), B("IOT", 0, 160), cc(6), A.is_equal, 256.0, A.mult)
+    ts(B("WJT", 0, 160), B("IOT", 0, 160), 16.0, A.subtract, cc(9), A.is_equal)
+    ts(S("MK", 0, 16), S("IOT", 0, 16), PS, A.is_equal)
+    ts(S("MS", 0, 8), S("IOT", 0, 8), PG, A.is_equal)
+    for t in range(ROUNDS):
+        ts(S("ZF", 32 + 8 * t, 40 + 8 * t), S("IOT", 0, 8), 16.0, A.mult, W + 128.0 * t, A.add)
+    for c in range(4):
         ts(B("SU1", c), B("DIV4", 0), float(c), A.subtract, cc(8), A.is_equal)
+    ts(S("KC", 0, 32), S("ZF", 32, 64), PS, A.add)
+    ts(cc(4), PS, 8.0, A.is_ge)
+    ts(cc(5), PS, 3.0, A.not_equal, 400.0, A.mult)
+    ts(cc(7), cc(4), -8.0, A.mult, PF, A.add)
+    ts(cc(14), PG, 2.0, A.mult, cc(5), A.add)
+    ts(cc(8), cc(4), 400.0, A.mult, cc(7), A.add)
+    ts(cc(15), cc(4), -400.0, A.mult, 400.0, A.add)
+    for c in range(2):
+        ts(B("SV3", c), B("DIV8", 0), float(c), A.subtract, cc(14), A.is_equal)
+    tt(cc(15), cc(15), cc(7), A.add)
     cp(S("NL", 0, 16), S("PR", 0, 16))
     for h in range(2):
-        ts(B("UC", h, 384), B("CM", h, 384), 4.0, A.mult, 34.0, A.add)
-        tt(B("FX", h, 384), B("UC", h, 384), B("VJ", h, 384), A.mult)
-        ts(B("FC", h, 384), B("FX", h, 384), 6, A.logical_shift_right, 2047, A.bitwise_and)
+        for c in range(2):
+            ts(B("SU3", 2 * h + c), B("IOT", 0), 8.0 * c, A.subtract, cc(8 + 7 * h), A.is_equal)
     act(S("W8F", 0, 8), S("B8", 0, 8), F.Copy, 0.0, BIG)
     act(S("W8A", 0, 8), S("B8", 0, 8), F.Copy, 0.0, 64.0)
     act(B("W1F", 0), B("BLK", 0), F.Copy, 0.0, BIG)
@@ -211,21 +237,13 @@ def rank_program(g, core, T, topo):
     act(B("BB", 0), B("MOD16", 0), F.Copy, 0.0, 1.0 / 128)
 
     def late_constants():
-        ts(B("IDb", 0), B("IOT", 0), PF, A.is_equal)
-        ts(B("WIT", 0, 160), B("IOT", 0, 160), cc(6), A.is_equal, 256.0, A.mult)
-        ts(B("WJT", 0, 160), B("IOT", 0, 160), 16.0, A.subtract, cc(9), A.is_equal)
-        ms(S("cc", 10, 11, 1, 0, 64), 32768.0)
-        ms(S("cc", 10, 11, 1, 64, 128), -120.0)
-        ts(B("CIT", 0, 160), B("MOD20", 0, 160), 16.0, A.is_lt, cc(10), A.mult)
-        ts(S("MK", 0, 16), S("IOT", 0, 16), PS, A.is_equal)
-        ts(S("MS", 0, 8), S("IOT", 0, 8), PG, A.is_equal)
-        ts(B("DRM", 0), B("MOD16", 0), 0.0, A.is_equal, float(2 ** 26), A.mult)
-        ts(B("DRS", 0, 160), B("MOD20", 0, 160), 0.5, A.is_gt)
         ts(S("PP", 0, 8), S("PR", 0, 8), 1024.0, A.mult, 1024.0, A.add)
-        for t in range(ROUNDS):
-            ts(S("ZF", 32 + 8 * t, 40 + 8 * t), S("IOT", 0, 8), 16.0, A.mult, W + 128.0 * t, A.add)
+        ts(B("CFL", 0, 160), B("MOD20", 0, 160), 16.0, A.is_lt)
+        ts(B("DRM", 0), B("MOD16", 0), 0.0, A.is_equal, float(2 ** 26), A.mult)
         tt(S("PP", 8, 16), S("PP", 0, 8), S("PR", 8, 16), A.add)
-        ts(S("KC", 0, 32), S("ZF", 32, 64), PS, A.add)
+        ts(B("DRS", 0, 160), B("MOD20", 0, 160), 0.5, A.is_gt)
+        for t in range(ROUNDS):
+            act(B("CIT", t, 160), B("CFL", 0, 160), F.Copy, 0.0, cc(10 + t))
         for m in range(8):
             act(B("EE", m, 16), S("MK", 0, 16), F.Copy, 0.0, S("PP", 8 + m, 9 + m))
         mm(S("HH", 448, 456), B("EE", 0), S("MS", 0, 8), True, True)
@@ -236,17 +254,17 @@ def rank_program(g, core, T, topo):
 
     def late_places():
         cp(S("KRX", 16, 24), S("HH", 448, 456))
+        cp(S("CI", 0, 128), B("HH", 0))
         ts(S("KI", 0, 8), S("KRX", 16, 24), 1024.0, A.subtract)
+        ts(S("CI", 128, 256), S("CI", 0, 128), 2032, A.bitwise_and)
         ts(S("KI", 8, 16), S("KI", 0, 8), 10, A.logical_shift_right, 1023, A.bitwise_and)
         ts(S("KI", 16, 24), S("KI", 0, 8), 1023, A.bitwise_and)
+        ts(S("CI", 256, 384), S("CI", 0, 128), 15, A.bitwise_and)
         ts(S("KRX", 0, 8), S("KI", 8, 16), 2.0, A.mult, 17.0, A.add)
         ts(S("KRX", 8, 16), S("KI", 16, 24), 2.0, A.mult, 593.0, A.add)
-        ts(S("HZ", 0, W), S("HT", 0, W), 8388608.0, A.add, 8388608.0, A.subtract)
-        cp(S("CI", 0, 128), B("HH", 0))
-        ts(S("CI", 128, 256), S("CI", 0, 128), 2032, A.bitwise_and)
-        ts(S("CI", 256, 384), S("CI", 0, 128), 15, A.bitwise_and)
         cp(S("ZB", 0, W, 16), S("CI", 128, 256))
         cp(S("ZB", 1, W, 16), S("CI", 256, 384))
+        ts(S("HZ", 0, W), S("HT", 0, W), 8388608.0, A.add, 8388608.0, A.subtract)
 
     def vb_bias():
         mm(S("VB", 0, 512), B("ONE", 0), S("CB", 0, 512), True, False)
@@ -254,38 +272,55 @@ def rank_program(g, core, T, topo):
     def lists_a(t):
         if t > 0:
             cp(S("NL", 0, 16), S("MR%d" % (t - 1), 0, 16))
+        act(B("VO", 0), G(S("VJ", 0, 768), S("NL", 8, 16)), F.Copy, 0.0, 0.5)
         cp(B("G16", 0), G(B("RW%d" % t, 0, 1024), S("NL", 0, 8)))
-        cp(S("LST", 544, 672), G(S("FC", 0, 768), S("NL", 8, 16)))
-        act(B("U2", 0), G(S("UC", 0, 768), S("NL", 8, 16)))
-        for a in range(4):
-            mm(B("VB", a), B("SEL", a), B("G16", 0), False, a == 3)
+        if t > 0:
+            act(B("U2", 0), G(S("UC", 0, 768), S("NL", 8, 16)))
+        else:
+            ts(B("U2", 0), G(S("CM", 0, 768), S("NL", 8, 16)), 4.0, A.mult, 34.0, A.add)
+        for a in range(3):
+            mm(B("VB", a), B("SEL", a), B("G16", 0), False, False)
+        for c in range(2):
+            mm(S("VB", 384, 448), B("SV3", c), S("G16", c, 128, 2), False, c == 1)
+
+    def lists_b(t):
+        def needs(b0, b1):
+            for b in range(b0, b1):
+                o, i = S("ZR", b, W, 16), S("HZ", W + 128 * t, W + 128 * t + 128)
+                if t == 0 and b % 2 == 0:
+                    act(o, i)
+                else:
+                    cp(o, i)
+
+        tt(B("XI", 3), B("U2", 0), B("VO", 0), A.mult)
+        for a in range(3):
+            tt(B("XI", a), B("U2", 0), B("VB", a), A.mult)
+        needs(0, 8)
+        ts(S("XJ", 0, 512), S("XI", 0, 512), 5, A.logical_shift_right, 2047, A.bitwise_and)
+        needs(8, 16)
+        cp(S("LST", 0, 512), S("XJ", 0, 512))
+        if t == 0:
+            ts(S("UC", 0, 768), S("CM", 0, 768), 4.0, A.mult, 34.0, A.add)
+
+    def lists_c():
         for c in range(4):
             mm(S("MI", 0, 32), B("SU1", c), S("G16", c, 128, 4), c == 0, c == 3)
         mm(S("MI", 32, 64), B("ONE", 0), S("CB", 0, 32), True, False)
         for c in range(4):
             mm(S("MI", 32, 64), B("SV1", c), S("G16", c, 128, 4), False, c == 3)
+        for h in range(2):
+            for c in range(2):
+                mm(S("MI", 224 + 64 * h, 288 + 64 * h), B("SU3", 2 * h + c), S("U2", c, 128, 2), c == 0, c == 1)
 
-    def lists_b():
-        for a in range(4):
-            tt(B("XI", a), B("U2", 0), B("VB", a), A.mult)
-        ts(S("U1", 0, 32), S("MI", 0, 32), 4.0, A.mult, 34.0, A.add)
-        tt(S("XI", 512, 544), S("U1", 0, 32), S("MI", 32, 64), A.mult)
-        ts(S("XJ", 0, 544), S("XI", 0, 544), 5, A.logical_shift_right, 2047, A.bitwise_and)
-        cp(S("LST", 0, 544), S("XJ", 0, 544))
-
-    def needs_s(t):
-        for b in range(0, 16, 2):
-            act(S("ZR", b, W, 16), S("HZ", W + 128 * t, W + 128 * t + 128))
-
-    def needs_v(t):
-        for b in range(1, 16, 2):
-            cp(S("ZR", b, W, 16), S("HZ", W + 128 * t, W + 128 * t + 128))
+    def names(t):
+        mm(S("MI", 64, 224), B("ONE", 0), B("CIT", t, 160), True, False)
+        mm(S("MI", 64, 224), B("U2", 0), B("WIT", 0, 160), False, False)
+        mm(S("MI", 64, 224), B("G16", 0), B("WJT", 0, 160), False, True)
 
     vb_bias()
     lists_a(0)
-    needs_s(0)
-    lists_b()
-    needs_v(0)
+    lists_b(0)
+    lists_c()
     for t in range(ROUNDS):
         dst = T.cores[(rank + 1 + t % 3) % N]
         src = T.cores[(rank - 1 - t % 3) % N]
@@ -297,33 +332,42 @@ def rank_program(g, core, T, topo):
         mm(B("S2", 0), B("ONE", 0), B("BB", 0), True, False)
         for a in range(4):
             mm(B("A%d" % a, 0), B("ONE", 0), B("BA", a), True, False)
+        if t > 0:
+            names(t)
         for name, off, cols, pos in CHUNKS:
             o, n = S("LST", off, off + cols), 16 * cols
+            if name == "a0":
+                act(B("UP", 0), S("MI", 224, 352))
+                act(S("U1", 0, 32), S("MI", 0, 32), F.Copy, 34.0, 4.0)
             act(S("CD", pos, pos + n), G(S(win, 0, W), o))
-            tt(S("FD", pos, pos + n), G(S("WIN", 0, W), o), S("ZR", 0, W, 4) if name == "f1" else S("ZR", 0, W), A.is_lt)
+            tt(S("FD", pos, pos + n), G(S("WIN", 0, W), o), S("ZR", 0, W, W // n), A.is_lt)
+            if name == "a0":
+                tt(S("XI", 512, 544), S("U1", 0, 32), S("MI", 32, 64), A.mult)
+                for h in range(2):
+                    tt(S("XI", 544 + 64 * h, 608 + 64 * h), B("UP", h, 64), S("VB", 384, 448), A.mult)
+            if name == "a1":
+                ts(S("XJ", 512, 672), S("XI", 512, 672), 5, A.logical_shift_right, 2047, A.bitwise_and)
+            if name == "a2":
+                cp(S("LST", 512, 672), S("XJ", 512, 672))
             if name == "f1":
                 for a in range(4):
                     mm(B("A%d" % a, 0), S("CD", pos + a, pos + n, 4), B("W1A", 0), False, False)
-                    mm(B("A%d" % a, 0), S("FD", pos + a, pos + n, 4), B("W1F", 0), False, False)
-                if t == 0:
-                    late_constants()
-                mm(S("MI", 64, 224), B("ONE", 0), B("CIT", 0, 160), True, False)
-                mm(S("MI", 64, 224), B("U2", 0), B("WIT", 0, 160), False, False)
-                mm(S("MI", 64, 224), B("G16", 0), B("WJT", 0, 160), False, True)
+                    mm(B("A%d" % a, 0), S("FD", pos + a, pos + n, 4), B("W1F", 0), False, a < 3)
                 continue
             bank = "S2" if name == "f2" else "A" + name[1]
-            for b in range(16):
-                mm(S(bank, b, 128, 16), S("FD", pos + b, pos + n, 16), S("W8F", 0, 8), False, False)
-            for b in range(16):
-                mm(S(bank, b, 128, 16), S("CD", pos + b, pos + n, 16), S("W8A", 0, 8), False, b == 15)
-            if name == "a0" and t == 0:
+            nb, b0 = n // 128, 8 if off == 608 else 0
+            for b in range(nb):
+                mm(S(bank, b0 + b, 128, 16), S("FD", pos + b, pos + n, nb), S("W8F", 0, 8), False, False)
+            for b in range(nb):
+                mm(S(bank, b0 + b, 128, 16), S("CD", pos + b, pos + n, nb), S("W8A", 0, 8), False, b0 + b == 15 and name in ("f2", "a3"))
+            if t == 0 and name == "a0":
+                late_constants()
+                names(t)
+            if t == 0 and name == "a2":
                 late_places()
-            if name == "a1":
-                act(B("R", 0), B("A0", 0))
-            if name == "a2":
-                tt(B("R", 1), B("R", 0), B("A1", 0), A.min)
-            if name == "a3":
-                tt(B("R", 2), B("R", 1), B("A2", 0), A.min)
+        act(B("R", 0), B("A0", 0))
+        tt(B("R", 1), B("R", 0), B("A1", 0), A.min)
+        tt(B("R", 2), B("R", 1), B("A2", 0), A.min)
 
         tt(B("R", 3), B("R", 2), B("A3", 0), A.min)
         tt(B("TT", 0), B("R", 3), B("S2", 0), A.add)
@@ -333,19 +377,21 @@ def rank_program(g, core, T, topo):
         cp(S("MI32", 0, 8), m8)
         for q in range(8):
             o, i, col = S("OH", 20 * q, 20 * q + 16), B("TT", q, 16), S("MC", 8 * t + q, 8 * t + q + 1)
-            if q < 3:
-                ts(o, i, 1.0, A.add, col, A.is_equal)
-            else:
+            if q >= 3:
                 act(o, i, F.Relu, col, -1.0)
-        ts(S("MI32", 8, 16), S("MI32", 0, 8), 4, A.logical_shift_right, 3, A.bitwise_and)
+                continue
+            ts(o, i, 1.0, A.add, col, A.is_equal)
+            if q == 0:
+                ts(S("MI32", 8, 16), S("MI32", 0, 8), 4, A.logical_shift_right, 3, A.bitwise_and)
         for a in range(4):
             ts(S("OH", 16 + a, 160, 20), S("MI32", 8, 16), float(a), A.is_equal)
         tt(B("PW", 0, 160), B("OH", 0, 160), S("MI", 64, 224), A.mult)
         scan(B("SC2", 0, 160), B("DRS", 0, 160), B("PW", 0, 160), 0.0, A.mult, A.add)
-        tt(S("PP", 8, 16), S("SC2", 19, 160, 20), S(kr, 16, 24), A.max)
+        msg, km, flag = "MSG%d" % t, "KM%d" % t, FLAG * (t + 1)
+        tt(S(km, 16, 24), S("SC2", 19, 160, 20), S(kr, 16, 24), A.max)
         for q in range(8):
-            o, col = B("EE", q, 16), S("PP", 8 + q, 9 + q)
-            if q < 5:
+            o, col = B("EE", q, 16), S(km, 16 + q, 17 + q)
+            if q < 3:
                 ts(o, S("MK", 0, 16), col, A.mult)
             else:
                 act(o, S("MK", 0, 16), F.Copy, 0.0, col)
@@ -353,63 +399,72 @@ def rank_program(g, core, T, topo):
         mm(LQ, B("EE", 0), S("MS", 0, 8), True, True)
         if not last:
             vb_bias()
-        msg, km = "MSG%d" % t, "KM%d" % t
-        ts(S("KI", 0, 8), S("PP", 8, 16), 1024.0, A.subtract)
-        ts(S("NG", 0, 8), S("PP", 8, 16), FLAG, A.is_lt, 64.0, A.mult)
+        ts(S("KI", 0, 8), S(km, 16, 24), 1024.0, A.subtract)
+        ts(S("NG", 0, 8), S(km, 16, 24), flag, A.is_ge)
         ts(S("KI", 8, 16), S("KI", 0, 8), 10, A.logical_shift_right, 1023, A.bitwise_and)
         ts(S("KI", 16, 24), S("KI", 0, 8), 1023, A.bitwise_and)
         ts(S(km, 0, 8), S("KI", 8, 16), 2.0, A.mult, 17.0, A.add)
         ts(S(km, 8, 16), S("KI", 16, 24), 2.0, A.mult, 593.0, A.add)
-        tt(S("XC", 0, 8), S(kr, 0, 8), S(km, 8, 16), A.mult)
-        ts(S("LI", 0, 8), LQ, 1024.0, A.subtract)
         tt(S("XC", 8, 16), S(km, 0, 8), S(kr, 8, 16), A.mult)
+        tt(S("XC", 0, 8), S(kr, 0, 8), S(km, 8, 16), A.mult)
         tt(S("XC", 16, 24), S(km, 0, 8), S(km, 8, 16), A.mult)
+        ts(S("LHI", 24, 48), S("XC", 0, 24), 12, A.logical_shift_right, 15, A.bitwise_and)
+        ts(S("LI", 0, 8), LQ, 1024.0, A.subtract)
+        ts(S("LHI", 0, 24), S("XC", 0, 24), 5, A.logical_shift_right, 127, A.bitwise_and)
         ts(S(msg, 0, 8), S("LI", 0, 8), 10, A.logical_shift_right, 1023, A.bitwise_and)
         ts(S(msg, 8, 16), S("LI", 0, 8), 1023, A.bitwise_and)
         send(S("MR%d" % t, 0, 16), S(msg, 0, 16), dst, "rn%d" % t, "ln%d" % t)
         recv(S("MR%d" % t, 0, 16), src, "rn%d" % t)
-        ts(S("LHI", 24, 48), S("XC", 0, 24), 12, A.logical_shift_right, 15, A.bitwise_and)
-        ts(S("LHI", 0, 24), S("XC", 0, 24), 5, A.logical_shift_right, 127, A.bitwise_and)
-        ts(S("ZF", 8, 16), LQ, FLAG, A.is_lt)
-        for c in range(3):
-            tt(S("LHF", 24 + 8 * c, 32 + 8 * c), S("LHI", 24 + 8 * c, 32 + 8 * c), S("NG", 0, 8), A.add)
-        cp(S("LHF", 0, 24), S("LHI", 0, 24))
-        ts(S("ZF", 16, 24), S(msg, 0, 8), 2.0, A.mult, 17.0, A.add)
-        ts(S("ZF", 24, 32), S(msg, 8, 16), 2.0, A.mult, 593.0, A.add)
-        tt(S("ZI", 0, 8), S("ZF", 16, 24), S("ZF", 24, 32), A.mult)
-        ts(S("ZI", 8, 16), S("ZI", 0, 8), 5, A.logical_shift_right, 2047, A.bitwise_and)
-        tt(S("ZF", 32, 40), S("ZF", 8, 16), B("KC", t, 8), A.mult)
-        tt(S("ZF", 40, 48), S("ZI", 8, 16), S("ZF", 32, 40), A.max)
-        cp(S("OFF", 0, 8), S("ZF", 40, 48))
-        cp(B("ZS%d" % t, 0), G(S("HZ", 0, zs + 128), S("OFF", 0, 8)))
-        send(S("HZ", zs + 128, zs + 256), B("ZS%d" % t, 0), dst, "rz%d" % t, "lz%d" % t)
-        recv(S("HZ", zs + 128, zs + 256), src, "rz%d" % t)
+        cp(S("LHF", 0, 48), S("LHI", 0, 48))
+
+        chain = [
+            lambda: ts(S("ZF", 8, 16), LQ, flag, A.is_lt),
+            lambda: ts(S("ZF", 16, 24), S(msg, 0, 8), 2.0, A.mult, 17.0, A.add),
+            lambda: ts(S("ZF", 24, 32), S(msg, 8, 16), 2.0, A.mult, 593.0, A.add),
+            lambda: tt(S("ZF", 32, 40), S("ZF", 8, 16), B("KC", t, 8), A.mult),
+            lambda: tt(S("ZI", 0, 8), S("ZF", 16, 24), S("ZF", 24, 32), A.mult),
+            lambda: ts(S("ZI", 8, 16), S("ZI", 0, 8), 5, A.logical_shift_right, 2047, A.bitwise_and),
+            lambda: tt(S("ZF", 40, 48), S("ZI", 8, 16), S("ZF", 32, 40), A.max),
+            lambda: cp(S("OFF", 0, 8), S("ZF", 40, 48)),
+            lambda: cp(B("ZS%d" % t, 0), G(S("HZ", 0, zs + 128), S("OFF", 0, 8))),
+            lambda: send(S("HZ", zs + 128, zs + 256), B("ZS%d" % t, 0), dst, "rz%d" % t, "lz%d" % t)]
+        step = 0
+        if not last:
+            for step in range(4):
+                chain[step]()
+            step = 4
         for h in range(2):
             for q in range(4 * h, 4 * h + 4):
                 for c in range(3):
                     n, m = 3 * q + c, 8 * c + q
                     act(B("SQ", n, 16), S("IOT", 0, 16), F.Square, S("LHF", 24 + m, 25 + m), -1.0)
-                    ts(B("OL", n), B("IOT", 0), S("LHF", m, m + 1), A.is_equal)
+                    ts(B("OL", n), B("IOT", 0), S("LHF", m, m + 1), A.is_equal, S("NG", q, q + 1), A.mult)
+                    if not last and step < len(chain):
+                        chain[step]()
+                        step += 1
             act(B("OHH", h, 192), B("SQ", h, 192), F.Relu, 4096.0, -4096.0)
             for q in range(4 * h, 4 * h + 4):
                 for c in range(3):
                     n = 3 * q + c
                     mm(S("HH", q, 128, 8), B("OL", n), B("OHH", n, 16), c == 0, c == 2)
+        recv(S("HZ", zs + 128, zs + 256), src, "rz%d" % t)
         if not last:
-            ts(S("NG", 8, 16), S("PP", 8, 16), FLAG, A.is_ge, -FLAG, A.mult)
-            tt(S(km, 16, 24), S("PP", 8, 16), S("NG", 8, 16), A.add)
             send(S("KR%d" % t, 0, 24), S(km, 0, 24), dst, "rk%d" % t, "lk%d" % t)
             recv(S("KR%d" % t, 0, 24), src, "rk%d" % t)
             lists_a(t + 1)
-            needs_s(t + 1)
         else:
-            ts(S("CK", 0, 32), S("MC", 0, 32), 1.0, A.subtract)
-            ts(S("CK", 32, 64), S("MC", 0, 32), BIG, A.is_lt)
-            cp(S("CKI", 0, 32), S("CK", 0, 32))
-            ts(S("CKI", 32, 64), S("CKI", 0, 32), 6, A.logical_shift_right)
-            ts(S("CK", 64, 96), S("CKI", 32, 64), 1.0, A.add)
-            tt(S("CK", 96, 128), S("CK", 64, 96), S("CK", 32, 64), A.mult)
-            ts(S("CK", 0, 32), S("CK", 96, 128), 1.0, A.subtract)
+            other = [
+                lambda: ts(S("CK", 0, 32), S("MC", 0, 32), 1.0, A.subtract),
+                lambda: ts(S("CK", 32, 64), S("MC", 0, 32), BIG, A.is_lt),
+                lambda: cp(S("CKI", 0, 32), S("CK", 0, 32)),
+                lambda: ts(S("CKI", 32, 64), S("CKI", 0, 32), 6, A.logical_shift_right),
+                lambda: ts(S("CK", 64, 96), S("CKI", 32, 64), 1.0, A.add),
+                lambda: tt(S("CK", 96, 128), S("CK", 64, 96), S("CK", 32, 64), A.mult),
+                lambda: ts(S("CK", 0, 32), S("CK", 96, 128), 1.0, A.subtract)]
+            for i in range(len(chain)):
+                chain[i]()
+                if i >= 2 and i - 2 < len(other):
+                    other[i - 2]()
         for d in range(1 if last else 2):
             tt(S("ZB", d, W, 16), S("ZB", d, W, 16), B("HH", 0), A.subtract)
         if last:
@@ -422,6 +477,12 @@ def rank_program(g, core, T, topo):
         for h in range(16):
             mm(B("A%d" % (h // 4), h % 4), B("ZB", h), B("IDb", 0), True, True)
         if last:
+            mm(S("S2", 0, 128, 1, 0, 32), S("CK", 0, 32), B("IDf", 0), True, True)
+            act(S("YC", 0, 128, 1, 0, 32), S("S2", 0, 128, 1, 0, 32))
+            cp(S("YP", 0, 16), S("MR3", 0, 16))
+            dmas("s", "op", [(X(T.yp[:]), S("YP", 0, 16))])
+            dmas("s", "oz", [(X(T.yz[:]), S("HZ", W + 512, W + 640))])
+            dmas("s", "oc", [(X(T.yc[:, 128 * q:128 * q + 128]), S("YC", 0, 128, 1, 8 * q, 8 * q + 8)) for q in range(ROUNDS)])
             for h in range(4):
                 tt(B("YF", h, 512), B("WIN", h, 512), S("A%d" % h, 0, 512), A.mult)
                 if h == 0:
@@ -429,17 +490,10 @@ def rank_program(g, core, T, topo):
                 else:
                     dmas("y", "oy%d" % h, [(X(T.yf[:, 512 * h - SHIFT:512 * h + 512 - SHIFT]), B("YF", h, 512))])
         else:
-            for h in range(3):
+            for h in range(4):
                 act(B("CW", h, 512), S("A%d" % h, 0, 512), F.Relu)
-            lists_b()
-            needs_v(t + 1)
-            ts(B("CW", 3, 512), S("A3", 0, 512), 0.0, A.max)
+            lists_b(t + 1)
+            lists_c()
 
-    mm(S("S2", 0, 128, 1, 0, 32), S("CK", 0, 32), B("IDf", 0), True, True)
-    act(S("YC", 0, 128, 1, 0, 32), S("S2", 0, 128, 1, 0, 32))
-    cp(S("YP", 0, 16), S("MR3", 0, 16))
-    dmas("s", "oc", [(X(T.yc[:, 128 * t:128 * t + 128]), S("YC", 0, 128, 1, 8 * t, 8 * t + 8)) for t in range(ROUNDS)])
-    dmas("s", "oz", [(X(T.yz[:]), S("HZ", W + 512, W + 640))])
-    dmas("s", "op", [(X(T.yp[:]), S("YP", 0, 16))])
     for s in sorted(final):
         g.wait_ge(T.sem[s], final[s])

from concourse.mybir import AluOpType as A, ActivationFunctionType as F

N, W, ROUNDS = 8, 2048, 4
SHIFT = 315
BIG = float(2 ** 19)
FLAG = float(2 ** 21)

SPEC = {
    "bfloat16": "WIN 2048 CW 2048 HZ 2688 HT 2048 ZR 2048 FD 10752 CD 10752 OL 3072 OHH 384 KA 128 ZB 2048 YF 2048 IOT 160 MOD16 128 MOD20 160 "
                "DIV16 128 DIV8 128 DIV4 128 IDb 128 BLK 128 W1F 128 W1A 128 B8 8 W8F 8 W8A 8 ONE 128 BA 512 BB 128 CB 512 CIT 640 CFL 160 "
                "ZS0 128 ZS1 128 ZS2 128 ZS3 128",
    "float32": "UC 768 VJ 768 VO 128 U2 128 U1 32 UP 128 SU3 512 R 512 TT 128 MSC 128 MC 32 OH 160 PW 160 SC2 160 PP 16 EE 128 ZF 64 NG 16 LHF 48 SQ 384 "
               "YP 16 YC 128 CK 128 pF 4 cc 16 IDf 128 WIT 160 MK 16 MS 8 DRM 128 DRS 160 KC 32 KM0 24 KM1 24 KM2 24 KM3 24 KR0 24 KR1 24 KR2 24 KRX 24",
    "int32": "CM 768 PR 16 XI 672 XJ 672 MI32 16 LI 8 ZI 16 KI 32 XC 24 LHI 48 CKI 64 CI 384 pI 4 RW0 1024 RW1 1024 RW2 1024 RW3 1024 "
             "MSG0 16 MSG1 16 MSG2 16 MSG3 16 MR0 16 MR1 16 MR2 16 MR3 16",
    "float16": "G16 128 SEL 512 SV1 512 SU1 512 SV3 256 WJT 160",
    "uint16": "NL 16 LST 672 OFF 8",
}
PSUM = ("A0", "A1", "A2", "A3", "S2", "VB", "MI", "HH")
SCRATCH = {n: ("psum", [128, 512], "float32") for n in PSUM}
for _ty, _l in SPEC.items():
    _l = _l.split()
    for _n, _c in zip(_l[::2], _l[1::2]):
        SCRATCH[_n] = ("sbuf", [128, int(_c)], _ty)
SEMAPHORES = ["qv", "qs", "qt", "qg", "dl", "dc", "dd", "df", "dn", "dr0", "dr1", "dr2", "dr3", "oy0", "oy1", "oy2", "oy3", "oc", "op", "oz"] + \
    [p + str(t) for p in ("rn", "rz", "rk", "ln", "lz", "lk") for t in range(ROUNDS)]
CHUNKS = [("f2", 384, 128, 0), ("a0", 0, 128, 2560), ("a1", 128, 128, 4608), ("a2", 256, 128, 6656), ("f1", 512, 32, 2048), ("a3", 544, 64, 8704), ("a3", 608, 64, 9728)]


def rank_program(g, core, T, topo):
    rank = T.rank_of(core)
    if rank is None:
        return
    queues = {"v": g.vector, "s": g.scalar, "t": g.tensor, "g": g, "y": g.sync}
    acc, cnt, final = {}, {}, {}
    known = {q: {} for q in "vstgyx"}

    def overlap(a, b):
        if max(a[1], b[1]) >= min(a[2], b[2]):
            return False
        if a[3] == b[3]:
            return a[3] == 1 or (a[1] - b[1]) % a[3] == 0
        if a[3] < b[3]:
            a, b = b, a
        return any(x in range(b[1], b[2], b[3]) for x in range(a[1], a[2], a[3]))

    def before(q, reads, writes):
        deps = {}
        for kind, regs in (("r", reads), ("w", writes)):
            for r in regs:
                for k2, r2, q2, ev, clk in acc.get(r[0], ()):
                    both = kind == "r" and k2 == "r"
                    if r[0] in PSUM:
                        if q == q2 and (q == "t" or both or not overlap(r, r2)):
                            continue
                    elif both or not overlap(r, r2):
                        continue
                    if known[q].get(ev[0], 0) < ev[1] and (ev[0] not in deps or deps[ev[0]][0] < ev[1]):
                        deps[ev[0]] = (ev[1], clk)
        for s in sorted(deps):
            if not any(s2 != s and deps[s2][1].get(s, 0) >= deps[s][0] for s2 in deps):
                queues[q].wait_ge(T.sem[s], deps[s][0])
        for s in deps:
            for s2, v in list(deps[s][1].items()) + [(s, deps[s][0])]:
                known[q][s2] = max(known[q].get(s2, 0), v)

    def after(q, reads, writes, ev):
        clk = dict(known[q])
        clk[ev[0]] = max(clk.get(ev[0], 0), ev[1])
        for kind, regs in (("r", reads), ("w", writes)):
            for r in regs:
                keep = []
                for e in acc.get(r[0], ()):
                    inside = r[1] <= e[1][1] and e[1][2] <= r[2] and (r[3] == 1 or (r[3] == e[1][3] and (r[1] - e[1][1]) % r[3] == 0))
                    if not (inside and (kind == "w" or (e[0] == "r" and e[2] == q))):
                        keep.append(e)
                acc[r[0]] = keep + [(kind, r, q, ev, clk)]

    def emit(q, call, reads, writes):
        before(q, reads, writes)
        s = "q" + q
        cnt[s] = cnt.get(s, 0) + 1
        call().then_inc(T.sem[s], 1)
        final[s] = cnt[s]
        after(q, reads, writes, (s, cnt[s]))

    def dmas(q, sem, moves):
        total = 16 * len(moves)
        for out, in_ in moves:
            before(q, in_[1], out[1])
            queues[q].dma_start(out[0], in_[0]).then_inc(T.sem[sem], 16)
        for out, in_ in moves:
            after(q, in_[1], out[1], (sem, total))
        final[sem] = total

    def S(name, a, b, step=1, p0=0, p1=128):
        t = T[name]
        return (t[p0:p1, a:b] if step == 1 else t[p0:p1, a:b:step], [(name, a, b, step)])

    def B(name, i, n=128):
        return S(name, n * i, n * i + n)

    def X(ap):
        return (ap, [])

    def G(win, off):
        return (win[0].indirect(off[0]), win[1] + off[1])

    def sc(x):
        return x[0] if isinstance(x, tuple) else x

    def rg(*xs):
        r = []
        for x in xs:
            r = r + (x[1] if isinstance(x, tuple) else [])
        return r

    def cp(out, in_):
        emit("v", lambda: g.vector.tensor_copy(out[0], in_[0]), in_[1], out[1])

    def tt(out, a, b, op):
        emit("v", lambda: g.vector.tensor_tensor(out[0], a[0], b[0], op), a[1] + b[1], out[1])

    def ts(out, a, s1, op0, s2=None, op1=None):
        if op1 is None:
            emit("v", lambda: g.vector.tensor_scalar(out[0], a[0], sc(s1), None, op0), rg(a, s1), out[1])
        else:
            emit("v", lambda: g.vector.tensor_scalar(out[0], a[0], sc(s1), sc(s2), op0, op1), rg(a, s1, s2), out[1])

    def ms(out, c):
        emit("v", lambda: g.vector.memset(out[0], c), [], out[1])

    def scan(out, a, b, init, op0, op1):
        emit("v", lambda: g.vector.tensor_tensor_scan(out[0], a[0], b[0], init, op0, op1), rg(a, b), out[1])

    def act(out, in_, func=F.Copy, bias=0.0, scale=1.0):
        emit("s", lambda: g.scalar.activation(out[0], in_[0], func, bias=sc(bias), scale=sc(scale)), rg(in_, bias, scale), out[1])

    def mm(out, lhsT, rhs, start, stop):
        emit("t", lambda: g.tensor.matmul(out[0], lhsT[0], rhs[0], start, stop), lhsT[1] + rhs[1], out[1])

    def iota(out, pattern, base=0, cm=0):
        if SCRATCH[out[1][0][0]][2] == "int32":
            emit("g", lambda: g.iota(out[0], pattern, base, cm), [], out[1])
        else:
            emit("g", lambda: g.iota(out[0], pattern, base, cm, allow_small_or_imprecise_dtypes=True), [], out[1])

    def send(out, src, dst, rsem, lsem):
        before("g", src[1], [])
        rid, pid = topo.addr(dst, core)
        g.remote_dma(out[0], src[0], T.sem[rsem], T.sem[lsem], pid, rid, topo.mask(core, dst))
        final[lsem] = len(topo.engines(core, dst))

    def recv(out, src, rsem):
        final[rsem] = len(topo.engines(src, core))
        after("x", [], out[1], (rsem, final[rsem]))

    def load_mates(t):
        n = "RW%d" % t
        iota(B(n, 0, 1024), [[1, 1024]])
        dmas("y", "dr%d" % t, [((T[n][16 * q:16 * q + 4, :], [(n, 0, 1024, 1)]), X(T.rmate[16 * q + 4 * t:16 * q + 4 * t + 4, :])) for q in range(8)])

    dmas("y", "dl", [(S("PR", 0, 8), X(T.prow[:])), (S("PR", 8, 16), X(T.pcol[:]))])
    dmas("y", "dc", [(B("CM", 0, 384), X(T.cmate[:, 0:384]))])
    dmas("y", "dd", [(B("CM", 1, 384), X(T.cmate[:, 384:768]))])
    dmas("s", "dn", [(S("HZ", W, W + 128), X(T.need[:]))])
    iota(S("pI", 0, 1), [[0, 1]], 0, 1)
    iota(B("IOT", 0, 160), [[1, 160]])
    iota(B("DIV16", 0), [[1, 8], [0, 16]])
    iota(B("DIV8", 0), [[1, 16], [0, 8]])
    load_mates(0)
    iota(B("DIV4", 0), [[1, 32], [0, 4]])
    iota(S("VJ", 0, 768), [[2, 768]], 593)
    iota(B("MOD16", 0), [[0, 8], [1, 16]])
    iota(B("MOD20", 0, 160), [[0, 8], [1, 20]])
    iota(S("ZB", 0, W), [[0, W]])
    for t in range(1, ROUNDS):
        load_mates(t)
    PF, PG, PS = S("pF", 0, 1), S("pF", 1, 2), S("pF", 2, 3)

    def cc(i):
        return S("cc", i, i + 1)

    ms(B("ONE", 0), 1.0)
    ms(S("CB", 0, 512, 1, 0, 64), 4.0)
    ms(S("CB", 0, 512, 1, 64, 128), 81.0 / 128)
    ms(S("cc", 10, 14, 1, 64, 128), -120.0)
    for t in range(ROUNDS):
        ms(S("cc", 10 + t, 11 + t, 1, 0, 64), 32768.0 * (t + 1))
    ts(S("pI", 1, 2), S("pI", 0, 1), 4, A.logical_shift_right)
    ts(S("pI", 2, 3), S("pI", 0, 1), 15, A.bitwise_and)
    cp(S("pF", 0, 3), S("pI", 0, 3))
    ts(B("BLK", 0), B("DIV16", 0), PG, A.is_equal)
    ts(S("B8", 0, 8), S("IOT", 0, 8), PG, A.is_equal)
    for a in range(4):
        ts(cc(a), PS, float(a), A.is_equal)
    ts(cc(4), PS, 4.0, A.is_ge, 200.0, A.mult)
    ts(cc(5), PS, 15.0, A.is_lt, 200.0, A.mult)
    ts(cc(6), PG, 4.0, A.mult, PF, A.add)
    tt(cc(7), cc(4), PF, A.add)
    ts(cc(8), PG, 4.0, A.mult, cc(5), A.add)
    ts(cc(9), cc(4), 2.0, A.mult, cc(6), A.add)
    for a in range(4):
        ts(B("SEL", a), B("BLK", 0), cc(a), A.mult)
    for c in range(4):
        ts(B("SV1", c), B("IOT", 0), 4.0 * c, A.subtract, cc(7), A.is_equal)
    ts(B("IDb", 0), B("IOT", 0), PF, A.is_equal)
    ts(B("WIT", 0, 160), B("IOT", 0, 160), cc(6), A.is_equal, 256.0, A.mult)
    ts(B("WJT", 0, 160), B("IOT", 0, 160), 16.0, A.subtract, cc(9), A.is_equal)
    ts(S("MK", 0, 16), S("IOT", 0, 16), PS, A.is_equal)
    ts(S("MS", 0, 8), S("IOT", 0, 8), PG, A.is_equal)
    for t in range(ROUNDS):
        ts(S("ZF", 32 + 8 * t, 40 + 8 * t), S("IOT", 0, 8), 16.0, A.mult, W + 128.0 * t, A.add)
    for c in range(4):
        ts(B("SU1", c), B("DIV4", 0), float(c), A.subtract, cc(8), A.is_equal)
    ts(S("KC", 0, 32), S("ZF", 32, 64), PS, A.add)
    ts(cc(4), PS, 8.0, A.is_ge)
    ts(cc(5), PS, 3.0, A.not_equal, 400.0, A.mult)
    ts(cc(7), cc(4), -8.0, A.mult, PF, A.add)
    ts(cc(14), PG, 2.0, A.mult, cc(5), A.add)
    ts(cc(8), cc(4), 400.0, A.mult, cc(7), A.add)
    ts(cc(15), cc(4), -400.0, A.mult, 400.0, A.add)
    for c in range(2):
        ts(B("SV3", c), B("DIV8", 0), float(c), A.subtract, cc(14), A.is_equal)
    tt(cc(15), cc(15), cc(7), A.add)
    cp(S("NL", 0, 16), S("PR", 0, 16))
    for h in range(2):
        for c in range(2):
            ts(B("SU3", 2 * h + c), B("IOT", 0), 8.0 * c, A.subtract, cc(8 + 7 * h), A.is_equal)
    act(S("W8F", 0, 8), S("B8", 0, 8), F.Copy, 0.0, BIG)
    act(S("W8A", 0, 8), S("B8", 0, 8), F.Copy, 0.0, 64.0)
    act(B("W1F", 0), B("BLK", 0), F.Copy, 0.0, BIG)
    act(B("W1A", 0), B("BLK", 0), F.Copy, 0.0, 64.0)
    for a in range(4):
        act(B("BA", a), B("BLK", 0), F.Copy, a / 8.0, 0.0)
    dmas("s", "df", [(S("WIN", SHIFT, W), X(T.fig[:, 0:W - SHIFT])), (S("WIN", 0, SHIFT), X(T.fig[:, W - SHIFT:W]))])
    act(B("BB", 0), B("MOD16", 0), F.Copy, 0.0, 1.0 / 128)

    def late_constants():
        ts(S("PP", 0, 8), S("PR", 0, 8), 1024.0, A.mult, 1024.0, A.add)
        ts(B("CFL", 0, 160), B("MOD20", 0, 160), 16.0, A.is_lt)
        ts(B("DRM", 0), B("MOD16", 0), 0.0, A.is_equal, float(2 ** 26), A.mult)
        tt(S("PP", 8, 16), S("PP", 0, 8), S("PR", 8, 16), A.add)
        ts(B("DRS", 0, 160), B("MOD20", 0, 160), 0.5, A.is_gt)
        for t in range(ROUNDS):
            act(B("CIT", t, 160), B("CFL", 0, 160), F.Copy, 0.0, cc(10 + t))
        for m in range(8):
            act(B("EE", m, 16), S("MK", 0, 16), F.Copy, 0.0, S("PP", 8 + m, 9 + m))
        mm(S("HH", 448, 456), B("EE", 0), S("MS", 0, 8), True, True)
        for h in range(16):
            mm(B("HH", h, 8), B("WIN", h), S("B8", 0, 8), True, True)
        act(S("HT", 0, W), S("WIN", 0, W), F.Copy, -0.25, 0.5)
        act(B("IDf", 0), B("IDb", 0))

    def late_places():
        cp(S("KRX", 16, 24), S("HH", 448, 456))
        cp(S("CI", 0, 128), B("HH", 0))
        ts(S("KI", 0, 8), S("KRX", 16, 24), 1024.0, A.subtract)
        ts(S("CI", 128, 256), S("CI", 0, 128), 2032, A.bitwise_and)
        ts(S("KI", 8, 16), S("KI", 0, 8), 10, A.logical_shift_right, 1023, A.bitwise_and)
        ts(S("KI", 16, 24), S("KI", 0, 8), 1023, A.bitwise_and)
        ts(S("CI", 256, 384), S("CI", 0, 128), 15, A.bitwise_and)
        ts(S("KRX", 0, 8), S("KI", 8, 16), 2.0, A.mult, 17.0, A.add)
        ts(S("KRX", 8, 16), S("KI", 16, 24), 2.0, A.mult, 593.0, A.add)
        cp(S("ZB", 0, W, 16), S("CI", 128, 256))
        cp(S("ZB", 1, W, 16), S("CI", 256, 384))
        ts(S("HZ", 0, W), S("HT", 0, W), 8388608.0, A.add, 8388608.0, A.subtract)

    def vb_bias():
        mm(S("VB", 0, 512), B("ONE", 0), S("CB", 0, 512), True, False)

    def lists_a(t):
        if t > 0:
            cp(S("NL", 0, 16), S("MR%d" % (t - 1), 0, 16))
        act(B("VO", 0), G(S("VJ", 0, 768), S("NL", 8, 16)), F.Copy, 0.0, 0.5)
        cp(B("G16", 0), G(B("RW%d" % t, 0, 1024), S("NL", 0, 8)))
        if t > 0:
            act(B("U2", 0), G(S("UC", 0, 768), S("NL", 8, 16)))
        else:
            ts(B("U2", 0), G(S("CM", 0, 768), S("NL", 8, 16)), 4.0, A.mult, 34.0, A.add)
        for a in range(3):
            mm(B("VB", a), B("SEL", a), B("G16", 0), False, False)
        for c in range(2):
            mm(S("VB", 384, 448), B("SV3", c), S("G16", c, 128, 2), False, c == 1)

    def lists_b(t):
        def needs(b0, b1):
            for b in range(b0, b1):
                o, i = S("ZR", b, W, 16), S("HZ", W + 128 * t, W + 128 * t + 128)
                if t == 0 and b % 2 == 0:
                    act(o, i)
                else:
                    cp(o, i)

        tt(B("XI", 3), B("U2", 0), B("VO", 0), A.mult)
        for a in range(3):
            tt(B("XI", a), B("U2", 0), B("VB", a), A.mult)
        needs(0, 8)
        ts(S("XJ", 0, 512), S("XI", 0, 512), 5, A.logical_shift_right, 2047, A.bitwise_and)
        needs(8, 16)
        cp(S("LST", 0, 512), S("XJ", 0, 512))
        if t == 0:
            ts(S("UC", 0, 768), S("CM", 0, 768), 4.0, A.mult, 34.0, A.add)

    def lists_c():
        for c in range(4):
            mm(S("MI", 0, 32), B("SU1", c), S("G16", c, 128, 4), c == 0, c == 3)
        mm(S("MI", 32, 64), B("ONE", 0), S("CB", 0, 32), True, False)
        for c in range(4):
            mm(S("MI", 32, 64), B("SV1", c), S("G16", c, 128, 4), False, c == 3)
        for h in range(2):
            for c in range(2):
                mm(S("MI", 224 + 64 * h, 288 + 64 * h), B("SU3", 2 * h + c), S("U2", c, 128, 2), c == 0, c == 1)

    def names(t):
        mm(S("MI", 64, 224), B("ONE", 0), B("CIT", t, 160), True, False)
        mm(S("MI", 64, 224), B("U2", 0), B("WIT", 0, 160), False, False)
        mm(S("MI", 64, 224), B("G16", 0), B("WJT", 0, 160), False, True)

    vb_bias()
    lists_a(0)
    lists_b(0)
    lists_c()
    for t in range(ROUNDS):
        dst = T.cores[(rank + 1 + t % 3) % N]
        src = T.cores[(rank - 1 - t % 3) % N]
        last = t == ROUNDS - 1
        kr = "KRX" if t == 0 else "KR%d" % (t - 1)
        win = "WIN" if t == 0 else "CW"
        zs = W + 128 * t

        mm(B("S2", 0), B("ONE", 0), B("BB", 0), True, False)
        for a in range(4):
            mm(B("A%d" % a, 0), B("ONE", 0), B("BA", a), True, False)
        if t > 0:
            names(t)
        for name, off, cols, pos in CHUNKS:
            o, n = S("LST", off, off + cols), 16 * cols
            if name == "a0":
                act(B("UP", 0), S("MI", 224, 352))
                act(S("U1", 0, 32), S("MI", 0, 32), F.Copy, 34.0, 4.0)
            act(S("CD", pos, pos + n), G(S(win, 0, W), o))
            tt(S("FD", pos, pos + n), G(S("WIN", 0, W), o), S("ZR", 0, W, W // n), A.is_lt)
            if name == "a0":
                tt(S("XI", 512, 544), S("U1", 0, 32), S("MI", 32, 64), A.mult)
                for h in range(2):
                    tt(S("XI", 544 + 64 * h, 608 + 64 * h), B("UP", h, 64), S("VB", 384, 448), A.mult)
            if name == "a1":
                ts(S("XJ", 512, 672), S("XI", 512, 672), 5, A.logical_shift_right, 2047, A.bitwise_and)
            if name == "a2":
                cp(S("LST", 512, 672), S("XJ", 512, 672))
            if name == "f1":
                for a in range(4):
                    mm(B("A%d" % a, 0), S("CD", pos + a, pos + n, 4), B("W1A", 0), False, False)
                    mm(B("A%d" % a, 0), S("FD", pos + a, pos + n, 4), B("W1F", 0), False, a < 3)
                continue
            bank = "S2" if name == "f2" else "A" + name[1]
            nb, b0 = n // 128, 8 if off == 608 else 0
            for b in range(nb):
                mm(S(bank, b0 + b, 128, 16), S("FD", pos + b, pos + n, nb), S("W8F", 0, 8), False, False)
            for b in range(nb):
                mm(S(bank, b0 + b, 128, 16), S("CD", pos + b, pos + n, nb), S("W8A", 0, 8), False, b0 + b == 15 and name in ("f2", "a3"))
            if t == 0 and name == "a0":
                late_constants()
                names(t)
            if t == 0 and name == "a2":
                late_places()
        act(B("R", 0), B("A0", 0))
        tt(B("R", 1), B("R", 0), B("A1", 0), A.min)
        tt(B("R", 2), B("R", 1), B("A2", 0), A.min)

        tt(B("R", 3), B("R", 2), B("A3", 0), A.min)
        tt(B("TT", 0), B("R", 3), B("S2", 0), A.add)
        scan(B("MSC", 0), B("DRM", 0), B("TT", 0), float(2 ** 26), A.add, A.min)
        m8 = S("MSC", 15, 128, 16)
        ts(B("MC", t, 8), m8, BIG - 1, A.min, 1.0, A.add)
        cp(S("MI32", 0, 8), m8)
        for q in range(8):
            o, i, col = S("OH", 20 * q, 20 * q + 16), B("TT", q, 16), S("MC", 8 * t + q, 8 * t + q + 1)
            if q >= 3:
                act(o, i, F.Relu, col, -1.0)
                continue
            ts(o, i, 1.0, A.add, col, A.is_equal)
            if q == 0:
                ts(S("MI32", 8, 16), S("MI32", 0, 8), 4, A.logical_shift_right, 3, A.bitwise_and)
        for a in range(4):
            ts(S("OH", 16 + a, 160, 20), S("MI32", 8, 16), float(a), A.is_equal)
        tt(B("PW", 0, 160), B("OH", 0, 160), S("MI", 64, 224), A.mult)
        scan(B("SC2", 0, 160), B("DRS", 0, 160), B("PW", 0, 160), 0.0, A.mult, A.add)
        msg, km, flag = "MSG%d" % t, "KM%d" % t, FLAG * (t + 1)
        tt(S(km, 16, 24), S("SC2", 19, 160, 20), S(kr, 16, 24), A.max)
        for q in range(8):
            o, col = B("EE", q, 16), S(km, 16 + q, 17 + q)
            if q < 3:
                ts(o, S("MK", 0, 16), col, A.mult)
            else:
                act(o, S("MK", 0, 16), F.Copy, 0.0, col)
        LQ = S("HH", 448, 456)
        mm(LQ, B("EE", 0), S("MS", 0, 8), True, True)
        if not last:
            vb_bias()
        ts(S("KI", 0, 8), S(km, 16, 24), 1024.0, A.subtract)
        ts(S("NG", 0, 8), S(km, 16, 24), flag, A.is_ge)
        ts(S("KI", 8, 16), S("KI", 0, 8), 10, A.logical_shift_right, 1023, A.bitwise_and)
        ts(S("KI", 16, 24), S("KI", 0, 8), 1023, A.bitwise_and)
        ts(S(km, 0, 8), S("KI", 8, 16), 2.0, A.mult, 17.0, A.add)
        ts(S(km, 8, 16), S("KI", 16, 24), 2.0, A.mult, 593.0, A.add)
        tt(S("XC", 8, 16), S(km, 0, 8), S(kr, 8, 16), A.mult)
        tt(S("XC", 0, 8), S(kr, 0, 8), S(km, 8, 16), A.mult)
        tt(S("XC", 16, 24), S(km, 0, 8), S(km, 8, 16), A.mult)
        ts(S("LHI", 24, 48), S("XC", 0, 24), 12, A.logical_shift_right, 15, A.bitwise_and)
        ts(S("LI", 0, 8), LQ, 1024.0, A.subtract)
        ts(S("LHI", 0, 24), S("XC", 0, 24), 5, A.logical_shift_right, 127, A.bitwise_and)
        ts(S(msg, 0, 8), S("LI", 0, 8), 10, A.logical_shift_right, 1023, A.bitwise_and)
        ts(S(msg, 8, 16), S("LI", 0, 8), 1023, A.bitwise_and)
        send(S("MR%d" % t, 0, 16), S(msg, 0, 16), dst, "rn%d" % t, "ln%d" % t)
        recv(S("MR%d" % t, 0, 16), src, "rn%d" % t)
        cp(S("LHF", 0, 48), S("LHI", 0, 48))

        chain = [
            lambda: ts(S("ZF", 8, 16), LQ, flag, A.is_lt),
            lambda: ts(S("ZF", 16, 24), S(msg, 0, 8), 2.0, A.mult, 17.0, A.add),
            lambda: ts(S("ZF", 24, 32), S(msg, 8, 16), 2.0, A.mult, 593.0, A.add),
            lambda: tt(S("ZF", 32, 40), S("ZF", 8, 16), B("KC", t, 8), A.mult),
            lambda: tt(S("ZI", 0, 8), S("ZF", 16, 24), S("ZF", 24, 32), A.mult),
            lambda: ts(S("ZI", 8, 16), S("ZI", 0, 8), 5, A.logical_shift_right, 2047, A.bitwise_and),
            lambda: tt(S("ZF", 40, 48), S("ZI", 8, 16), S("ZF", 32, 40), A.max),
            lambda: cp(S("OFF", 0, 8), S("ZF", 40, 48)),
            lambda: cp(B("ZS%d" % t, 0), G(S("HZ", 0, zs + 128), S("OFF", 0, 8))),
            lambda: send(S("HZ", zs + 128, zs + 256), B("ZS%d" % t, 0), dst, "rz%d" % t, "lz%d" % t)]
        step = 0
        if not last:
            for step in range(4):
                chain[step]()
            step = 4
        for h in range(2):
            for q in range(4 * h, 4 * h + 4):
                for c in range(3):
                    n, m = 3 * q + c, 8 * c + q
                    act(B("SQ", n, 16), S("IOT", 0, 16), F.Square, S("LHF", 24 + m, 25 + m), -1.0)
                    ts(B("OL", n), B("IOT", 0), S("LHF", m, m + 1), A.is_equal, S("NG", q, q + 1), A.mult)
                    if not last and step < len(chain):
                        chain[step]()
                        step += 1
            act(B("OHH", h, 192), B("SQ", h, 192), F.Relu, 4096.0, -4096.0)
            for q in range(4 * h, 4 * h + 4):
                for c in range(3):
                    n = 3 * q + c
                    mm(S("HH", q, 128, 8), B("OL", n), B("OHH", n, 16), c == 0, c == 2)
        recv(S("HZ", zs + 128, zs + 256), src, "rz%d" % t)
        if not last:
            send(S("KR%d" % t, 0, 24), S(km, 0, 24), dst, "rk%d" % t, "lk%d" % t)
            recv(S("KR%d" % t, 0, 24), src, "rk%d" % t)
            lists_a(t + 1)
        else:
            other = [
                lambda: ts(S("CK", 0, 32), S("MC", 0, 32), 1.0, A.subtract),
                lambda: ts(S("CK", 32, 64), S("MC", 0, 32), BIG, A.is_lt),
                lambda: cp(S("CKI", 0, 32), S("CK", 0, 32)),
                lambda: ts(S("CKI", 32, 64), S("CKI", 0, 32), 6, A.logical_shift_right),
                lambda: ts(S("CK", 64, 96), S("CKI", 32, 64), 1.0, A.add),
                lambda: tt(S("CK", 96, 128), S("CK", 64, 96), S("CK", 32, 64), A.mult),
                lambda: ts(S("CK", 0, 32), S("CK", 96, 128), 1.0, A.subtract)]
            for i in range(len(chain)):
                chain[i]()
                if i >= 2 and i - 2 < len(other):
                    other[i - 2]()
        for d in range(1 if last else 2):
            tt(S("ZB", d, W, 16), S("ZB", d, W, 16), B("HH", 0), A.subtract)
        if last:
            ts(B("KA", 0), S("ZB", 0, W, 16), 0.0, A.is_gt)
            for s in range(16):
                if s % 3 == 2:
                    act(S("ZB", s, W, 16), B("KA", 0), F.Copy, -1.0, 2.0)
                else:
                    ts(S("ZB", s, W, 16), B("KA", 0), 2.0, A.mult, -1.0, A.add)
        for h in range(16):
            mm(B("A%d" % (h // 4), h % 4), B("ZB", h), B("IDb", 0), True, True)
        if last:
            mm(S("S2", 0, 128, 1, 0, 32), S("CK", 0, 32), B("IDf", 0), True, True)
            act(S("YC", 0, 128, 1, 0, 32), S("S2", 0, 128, 1, 0, 32))
            cp(S("YP", 0, 16), S("MR3", 0, 16))
            dmas("s", "op", [(X(T.yp[:]), S("YP", 0, 16))])
            dmas("s", "oz", [(X(T.yz[:]), S("HZ", W + 512, W + 640))])
            dmas("s", "oc", [(X(T.yc[:, 128 * q:128 * q + 128]), S("YC", 0, 128, 1, 8 * q, 8 * q + 8)) for q in range(ROUNDS)])
            for h in range(4):
                tt(B("YF", h, 512), B("WIN", h, 512), S("A%d" % h, 0, 512), A.mult)
                if h == 0:
                    dmas("y", "oy0", [(X(T.yf[:, W - SHIFT:W]), S("YF", 0, SHIFT)), (X(T.yf[:, 0:512 - SHIFT]), S("YF", SHIFT, 512))])
                else:
                    dmas("y", "oy%d" % h, [(X(T.yf[:, 512 * h - SHIFT:512 * h + 512 - SHIFT]), B("YF", h, 512))])
        else:
            for h in range(4):
                act(B("CW", h, 512), S("A%d" % h, 0, 512), F.Relu)
            lists_b(t + 1)
            lists_c()

    for s in sorted(final):
        g.wait_ge(T.sem[s], final[s])
